import numpy as np, ml_dtypes
CORES = [88,96,104,112,120,216,224,232,240,248]
N = 10
TOK, CAP, FF = 512, 80, 4
def entries(a): return a.T.reshape(-1)
def pack(v, P): return np.ascontiguousarray(np.asarray(v, np.int32).reshape(-1, P).T)
def lists(rng, how):
    E = rng.integers(0, N, (N, TOK))
    if how == "hot": E[:] = rng.integers(N)
    if how == "none": E = (int(rng.integers(N)) + 1 + rng.integers(0, N - 1, (N, TOK))) % N
    if how == "skew": E = np.where(rng.random((N, TOK)) < 0.7, rng.integers(0, N, (N, 1)), E)
    if how == "even": E = np.stack([rng.permutation(np.arange(TOK) % N) for r in range(N)])
    if how == "own": E = np.repeat(np.arange(N).reshape(N, 1), TOK, axis=1)
    return {"ex": np.stack([pack(E[r], 16) for r in range(N)])}
def setup_inputs(rng):
    return dict({"x": rng.standard_normal((N, 128, TOK), dtype=np.float32).astype(ml_dtypes.bfloat16), "w1": (rng.standard_normal((N, 128, FF * 128), dtype=np.float32) / 8).astype(ml_dtypes.bfloat16), "w2": (rng.standard_normal((N, 128, FF * 128), dtype=np.float32) / 16).astype(ml_dtypes.bfloat16)}, **lists(rng, "uniform"))
def setup_inputs_even(rng):
    d = setup_inputs(rng); d.update(lists(rng, "even"))
    for k in ("x",): d[k] = (d[k].astype(np.float32) * 1024.0).astype(d[k].dtype)
    return d
def setup_inputs_hot(rng):
    d = setup_inputs(rng); d.update(lists(rng, "hot"))
    for k in ("x",): d[k] = (d[k].astype(np.float32) * (1 / 1024.0)).astype(d[k].dtype)
    return d
def setup_inputs_none(rng):
    d = setup_inputs(rng); d.update(lists(rng, "none"))
    return d
def setup_inputs_own(rng):
    d = setup_inputs(rng); d.update(lists(rng, "own"))
    return d
def setup_inputs_skew(rng):
    d = setup_inputs(rng); d.update(lists(rng, "skew"))
    return d
def check_inputs(x):
    bad = []
    if x["ex"].min() < 0 or x["ex"].max() >= N: bad.append("ex out of range")
    return bad
def reference(x, w1, w2, ex):
    X, W1, W2 = x.astype(np.float64), w1.astype(np.float64), w2.astype(np.float64)
    y = np.zeros((N, 128, TOK))
    for r in range(N):
        E = entries(ex[r]); place = np.array([np.sum(E[:t] == E[t]) for t in range(TOK)])
        for k in range(N):
            m = (E == k) & (place < CAP)
            y[r][:, m] = sum(W2[k][:, 128 * f:128 * f + 128].T @ np.maximum(W1[k][:, 128 * f:128 * f + 128].T @ X[r][:, m], 0.0) for f in range(FF))
    return {"y": y.astype(ml_dtypes.bfloat16)}

@@ -1,0 +1,319 @@
+import comms_topo
+from concourse.bass import DstId, RemoteDMATransfer
+from concourse.mybir import AluOpType, ActivationFunctionType
+
+NSIM = 256
+TOK, CAP, FF = 512, 80, 4
+NR = 10
+SLOTS = NR * CAP
+
+SCRATCH = {
+    "X": ("sbuf", [128, TOK], "bfloat16"),
+    "W": ("sbuf", [128, 2 * FF * 128], "bfloat16"),
+    "D": ("sbuf", [128, SLOTS + TOK], "bfloat16"),
+    "F": ("sbuf", [128, 2 * CAP], "bfloat16"),
+    "R": ("sbuf", [128, 2 * CAP], "bfloat16"),
+    "Hh": ("sbuf", [128, 2 * FF * CAP], "bfloat16"),
+    "Yo": ("sbuf", [128, 2 * CAP], "bfloat16"),
+    "Z": ("sbuf", [128, SLOTS + 8], "bfloat16"),
+    "Yf": ("sbuf", [128, TOK], "bfloat16"),
+    "E16": ("sbuf", [128, 32], "int32"),
+    "Ebf": ("sbuf", [128, 32], "bfloat16"),
+    "pI": ("sbuf", [128, 1], "int32"),
+    "gI": ("sbuf", [128, 1], "int32"),
+    "pF": ("sbuf", [128, 1], "float32"),
+    "eid": ("sbuf", [128, 2], "float32"),
+    "rowi": ("sbuf", [128, 1], "float32"),
+    "bca": ("sbuf", [128, 2], "float32"),
+    "bcb": ("sbuf", [128, 2], "float32"),
+    "bc": ("sbuf", [128, 2], "float32"),
+    "coli": ("sbuf", [128, 128], "bfloat16"),
+    "colg": ("sbuf", [128, 128], "bfloat16"),
+    "SEL": ("sbuf", [128, 128], "bfloat16"),
+    "ON": ("sbuf", [128, 128], "bfloat16"),
+    "LE": ("sbuf", [128, 128], "bfloat16"),
+    "M2": ("sbuf", [128, 128], "bfloat16"),
+    "SB0": ("sbuf", [128, 128], "bfloat16"),
+    "SB1": ("sbuf", [128, 128], "bfloat16"),
+    "T8a": ("sbuf", [128, 32], "float32"),
+    "T8": ("sbuf", [128, 32], "float32"),
+    "MSK": ("sbuf", [128, 64], "bfloat16"),
+    "O": ("sbuf", [128, 64], "bfloat16"),
+    "Sc": ("sbuf", [128, 64], "bfloat16"),
+    "R1": ("sbuf", [128, 64], "bfloat16"),
+    "R2": ("sbuf", [128, 64], "bfloat16"),
+    "OF": ("sbuf", [128, 32], "float32"),
+    "off1": ("sbuf", [128, 32], "uint16"),
+    "off2": ("sbuf", [128, 32], "uint16"),
+}
+for _b in range(8):
+    SCRATCH["B%d" % _b] = ("psum", [128, 512], "float32")
+
+SEMAPHORES = ["vs", "ps", "ss", "gs", "exl", "xl", "wl", "st", "lsem", "farr", "warr", "rarr0", "rarr1", "zarr"]
+
+_PLAN = {}
+
+
+def _bits(m):
+    return [1 << i for i in range(16) if (m >> i) & 1]
+
+
+def _split(m, n):
+    b = _bits(m)
+    w = len(b) // n
+    return [sum(b[i * w:(i + 1) * w]) for i in range(n)]
+
+
+def _plan(T, topo):
+    if "p" in _PLAN:
+        return _PLAN["p"]
+    cores = [int(c) for c in T.cores]
+    n = len(cores)
+    helpers = []
+    for c in cores:
+        hs = [h for h in range(NSIM) if h != c and topo.host(h) == topo.host(c) and topo.chip(h) == topo.chip(c)
+              and all(topo.may_write(h, d) for d in cores)]
+        helpers.append(hs[:4])
+    kd = [k for k in range(1, n, 2) if all(topo.may_write(cores[r], cores[(r + k) % n]) for r in range(n))][0]
+    rest = [k for k in range(1, n) if k != kd]
+    pairs = [(rest[2 * a], rest[2 * a + 1]) for a in range(4)]
+    role = {}
+    for r in range(n):
+        for a, h in enumerate(helpers[r]):
+            role[h] = (r, a)
+    _PLAN["p"] = (cores, helpers, kd, pairs, role)
+    return _PLAN["p"]
+
+
+def rank_program(g, core, T, topo):
+    cores, helpers, kd, pairs, role = _plan(T, topo)
+    n = len(cores)
+    rank = T.rank_of(core)
+    if rank is None and core not in role:
+        return
+    S = T.sem
+    Op = AluOpType
+    cnt = {"v": 0, "p": 0, "s": 0, "g": 0, "l": 0}
+
+    def V(fn):
+        if cnt["v"]:
+            g.vector.wait_ge(S.vs, cnt["v"])
+        fn().then_inc(S.vs, 1)
+        cnt["v"] += 1
+        return cnt["v"]
+
+    def P(fn):
+        if cnt["p"]:
+            g.tensor.wait_ge(S.ps, cnt["p"])
+        fn().then_inc(S.ps, 1)
+        cnt["p"] += 1
+        return cnt["p"]
+
+    def A(fn):
+        if cnt["s"]:
+            g.scalar.wait_ge(S.ss, cnt["s"])
+        fn().then_inc(S.ss, 1)
+        cnt["s"] += 1
+        return cnt["s"]
+
+    def G(fn):
+        if cnt["g"]:
+            g.wait_ge(S.gs, cnt["g"])
+        fn().then_inc(S.gs, 1)
+        cnt["g"] += 1
+        return cnt["g"]
+
+    def xfer(dst_core, mask, sem, src, dst):
+        rid, pid = topo.addr(dst_core, core)
+        cnt["l"] += len(_bits(mask))
+        return RemoteDMATransfer(dst_ids=[DstId(rid=rid, pnc=pid)], dma_engine_mask=mask, remote_sem=sem, src=src, dst=dst)
+
+    def send(dst_core, sem, src, dst):
+        rid, pid = topo.addr(dst_core, core)
+        mask = topo.mask(core, dst_core)
+        cnt["l"] += len(_bits(mask))
+        g.remote_dma(out_ap=dst, in_ap=src, remote_sem=sem, local_sem=S.lsem, pid=pid, routing_id=rid,
+                     dma_engine_mask=mask)
+        return len(_bits(mask))
+
+    mm = g.tensor.matmul
+    BK = [(T.B3, T.B4, T.B5), (T.B6, T.B7, T.B0)]
+    st = [{}, {}]
+
+    def mm1(b, rhs):
+        X, Y, _ = BK[b]
+        mm(X[:, 0:CAP], T.W[:, 0:128], rhs, True, True)
+        st[b]["x"] = P(lambda: mm(X[:, CAP:2 * CAP], T.W[:, 128:256], rhs, True, True))
+        mm(Y[:, 0:CAP], T.W[:, 256:384], rhs, True, True)
+        st[b]["y"] = P(lambda: mm(Y[:, CAP:2 * CAP], T.W[:, 384:512], rhs, True, True))
+
+    def relu(b):
+        X, Y, _ = BK[b]
+        o = b * FF * CAP
+        g.vector.wait_ge(S.ps, st[b]["x"])
+        st[b]["hv"] = V(lambda: g.vector.tensor_scalar(T.Hh[:, o:o + 2 * CAP], X[:, 0:2 * CAP], 0.0, None, Op.max))
+        g.scalar.wait_ge(S.ps, st[b]["y"])
+        st[b]["hs"] = A(lambda: g.scalar.activation(T.Hh[:, o + 2 * CAP:o + 4 * CAP], Y[:, 0:2 * CAP],
+                                                    ActivationFunctionType.Relu))
+
+    def mm2(b):
+        Zb = BK[b][2]
+        o = b * FF * CAP
+        g.tensor.wait_ge(S.vs, st[b]["hv"])
+        g.tensor.wait_ge(S.ss, st[b]["hs"])
+        for f in range(FF - 1):
+            mm(Zb[:, 0:CAP], T.W[:, 512 + 128 * f:640 + 128 * f], T.Hh[:, o + CAP * f:o + CAP * f + CAP], f == 0, False)
+        f = FF - 1
+        st[b]["z"] = P(lambda: mm(Zb[:, 0:CAP], T.W[:, 512 + 128 * f:640 + 128 * f],
+                                  T.Hh[:, o + CAP * f:o + CAP * f + CAP], False, True))
+
+    def out_v(b, dst):
+        g.vector.wait_ge(S.ps, st[b]["z"])
+        return V(lambda: g.vector.tensor_copy(dst, BK[b][2][:, 0:CAP]))
+
+    def out_s(b, dst):
+        g.scalar.wait_ge(S.ps, st[b]["z"])
+        return A(lambda: g.scalar.activation(dst, BK[b][2][:, 0:CAP], ActivationFunctionType.Copy))
+
+    def finish(extra):
+        for sem, val in extra + [(S.lsem, cnt["l"]), (S.vs, cnt["v"]), (S.ps, cnt["p"]), (S.ss, cnt["s"]),
+                                 (S.gs, cnt["g"])]:
+            if val:
+                g.wait_ge(sem, val)
+
+    if rank is None:
+        r, a = role[core]
+        k0, k1 = pairs[a]
+        d0, d1 = helpers[(r + k0) % n][a], helpers[(r + k1) % n][a]
+        m0, m1 = _split(topo.mask(core, d0) & topo.mask(core, d1), 2)
+        nf = len(_bits(_split(topo.mask(cores[r], core), 4)[a]))
+        g.wait_ge(S.farr, nf)
+        g.remote_dma_fused([xfer(d0, m0, S.rarr0, T.F[:, 0:CAP], T.R[:, 0:CAP]),
+                            xfer(d1, m1, S.rarr1, T.F[:, CAP:2 * CAP], T.R[:, CAP:2 * CAP])], local_sem=S.lsem)
+        g.tensor.wait_ge(S.warr, len(_bits(_split(topo.mask(cores[r], core), 2)[0])))
+        g.tensor.wait_ge(S.rarr0, len(_bits(m0)))
+        mm1(0, T.R[:, 0:CAP])
+        g.tensor.wait_ge(S.rarr1, len(_bits(m1)))
+        mm1(1, T.R[:, CAP:2 * CAP])
+        relu(0)
+        relu(1)
+        mm2(0)
+        mm2(1)
+        c0 = out_v(0, T.Yo[:, 0:CAP])
+        c1 = out_s(1, T.Yo[:, CAP:2 * CAP])
+        g.wait_ge(S.vs, c0)
+        send(cores[(r - k0) % n], S.zarr, T.Yo[:, 0:CAP], T.Z[:, CAP * k0:CAP * k0 + CAP])
+        g.wait_ge(S.ss, c1)
+        send(cores[(r - k1) % n], S.zarr, T.Yo[:, CAP:2 * CAP], T.Z[:, CAP * k1:CAP * k1 + CAP])
+        finish([])
+        return
+
+    r = rank
+    H = helpers[r]
+    ve = g.vector
+    g.sync.dma_start(T.E16[0:16, :], T.ex[:, :]).then_inc(S.exl, 16)
+    g.scalar.dma_start(T.X[:, :], T.x[:, :]).then_inc(S.xl, 16)
+    g.sync.dma_start(T.W[:, 0:512], T.w1[:, :]).then_inc(S.wl, 16)
+    g.scalar.dma_start(T.W[:, 512:1024], T.w2[:, :]).then_inc(S.wl, 16)
+
+    i_p = G(lambda: g.iota(T.pI[:, :], [[0, 1]], 0, 1))
+    i_f = G(lambda: g.iota(T.pF[:, :], [[0, 1]], 0, 1, allow_small_or_imprecise_dtypes=True))
+    i_ci = G(lambda: g.iota(T.coli[:, :], [[0, 8], [1, 16]], 0, 0, allow_small_or_imprecise_dtypes=True))
+    i_cg = G(lambda: g.iota(T.colg[:, :], [[1, 8], [0, 16]], 0, 0, allow_small_or_imprecise_dtypes=True))
+    i_t8 = G(lambda: g.iota(T.T8a[:, :], [[16, 32]], SLOTS, 0, allow_small_or_imprecise_dtypes=True))
+
+    V(lambda: ve.memset(T.D[:, 0:SLOTS], 0.0))
+    V(lambda: ve.memset(T.MSK[:, :], 1.0))
+    V(lambda: ve.memset(T.MSK[:, 32:33], 0.0))
+    V(lambda: ve.memset(T.Z[:, SLOTS:SLOTS + 8], 0.0))
+    ve.wait_ge(S.gs, i_p)
+    V(lambda: ve.tensor_scalar(T.gI[:, :], T.pI[:, :], 4, None, Op.arith_shift_right))
+    V(lambda: ve.tensor_copy(T.eid[:, 0:1], T.gI[:, :]))
+    V(lambda: ve.tensor_scalar(T.eid[:, 1:2], T.eid[:, 0:1], 8.0, None, Op.add))
+    ve.wait_ge(S.gs, i_f)
+    V(lambda: ve.tensor_scalar(T.rowi[:, :], T.eid[:, 0:1], -16.0, T.pF[:, 0:1], Op.mult, Op.add))
+    ve.wait_ge(S.gs, i_ci)
+    c_sel = V(lambda: ve.tensor_scalar(T.SEL[:, :], T.coli[:, :], T.rowi[:, 0:1], None, Op.is_equal))
+    ve.wait_ge(S.gs, i_cg)
+    V(lambda: ve.tensor_scalar(T.ON[:, :], T.colg[:, :], T.eid[:, 0:1], None, Op.is_equal))
+    V(lambda: ve.tensor_scalar(T.LE[:, :], T.coli[:, :], T.rowi[:, 0:1], -1.0, Op.is_le, Op.mult))
+    V(lambda: ve.tensor_tensor(T.M2[:, :], T.LE[:, :], T.ON[:, :], Op.mult))
+    V(lambda: ve.tensor_scalar(T.bca[:, :], T.eid[:, :], float(r), float(SLOTS), Op.is_lt, Op.mult))
+    V(lambda: ve.tensor_scalar(T.bcb[:, :], T.eid[:, :], float(CAP), float(-CAP * r), Op.mult, Op.add))
+    V(lambda: ve.tensor_tensor(T.bc[:, :], T.bca[:, :], T.bcb[:, :], Op.add))
+    V(lambda: ve.tensor_scalar(T.SB0[:, :], T.SEL[:, :], T.bc[:, 0:1], None, Op.mult))
+    V(lambda: ve.tensor_scalar(T.SB1[:, :], T.SEL[:, :], T.bc[:, 1:2], None, Op.mult))
+    ve.wait_ge(S.gs, i_t8)
+    V(lambda: ve.tensor_scalar(T.T8[:, :], T.T8a[:, :], T.rowi[:, 0:1], None, Op.add))
+
+    ve.wait_ge(S.exl, 16)
+    c = V(lambda: ve.tensor_copy(T.Ebf[0:16, :], T.E16[0:16, :]))
+    g.tensor.wait_ge(S.vs, c)
+    p = P(lambda: mm(T.B0[:, 0:32], T.SEL[0:16, :], T.Ebf[0:16, :], True, True))
+    ve.wait_ge(S.ps, p)
+    V(lambda: ve.tensor_scalar(T.O[:, 0:32], T.B0[:, 0:32], T.eid[:, 0:1], None, Op.is_equal))
+    c_o = V(lambda: ve.tensor_scalar(T.O[:, 32:64], T.B0[:, 0:32], T.eid[:, 1:2], None, Op.is_equal))
+    c_s = V(lambda: ve.tensor_tensor_scan(T.Sc[:, :], T.MSK[:, :], T.O[:, :], 0.0, Op.mult, Op.add))
+    g.tensor.wait_ge(S.vs, c_o)
+    mm(T.B1[:, 0:64], T.M2[:, :], T.O[:, :], True, False)
+    mm(T.B2[:, 0:32], T.SB0[:, :], T.O[:, 0:32], True, False)
+    mm(T.B2[:, 0:32], T.SB1[:, :], T.O[:, 32:64], False, False)
+    g.tensor.wait_ge(S.vs, c_s)
+    p = P(lambda: mm(T.B1[:, 0:64], T.ON[:, :], T.Sc[:, :], False, True))
+    ve.wait_ge(S.ps, p)
+    c_1 = V(lambda: ve.tensor_tensor(T.R1[:, :], T.B1[:, 0:64], T.O[:, :], Op.mult))
+    c_2 = V(lambda: ve.tensor_scalar(T.R2[:, :], T.R1[:, :], float(CAP), 4096.0, Op.is_ge, Op.mult))
+    g.tensor.wait_ge(S.vs, c_1)
+    mm(T.B2[:, 0:32], T.SEL[:, :], T.R1[:, 0:32], False, False)
+    mm(T.B2[:, 0:32], T.SEL[:, :], T.R1[:, 32:64], False, False)
+    g.tensor.wait_ge(S.vs, c_2)
+    mm(T.B2[:, 0:32], T.SEL[:, :], T.R2[:, 0:32], False, False)
+    p = P(lambda: mm(T.B2[:, 0:32], T.SEL[:, :], T.R2[:, 32:64], False, True))
+    ve.wait_ge(S.ps, p)
+    V(lambda: ve.tensor_tensor(T.OF[:, :], T.B2[:, 0:32], T.T8[:, :], Op.min))
+    V(lambda: ve.tensor_copy(T.off1[:, :], T.OF[:, :]))
+    ve.wait_ge(S.xl, 16)
+    c_d = V(lambda: ve.tensor_copy(T.D[:, 0:SLOTS + TOK].indirect(T.off1[:, 0:32]), T.X[:, :]))
+    V(lambda: ve.tensor_scalar(T.off2[:, :], T.OF[:, :], float(SLOTS), None, Op.min))
+
+    twin = cores[(r + kd) % n]
+    wm = _split(topo.mask(core, H[0]), 2)
+    g.wait_ge(S.wl, 32)
+    g.remote_dma_fused([xfer(H[0], wm[0], S.warr, T.W[:, :], T.W[:, :]),
+                        xfer(H[2], wm[1], S.warr, T.W[:, :], T.W[:, :])], local_sem=S.lsem)
+    g.wait_ge(S.vs, c_d)
+    dm = _split(topo.mask(core, H[0]), 4)
+    g.remote_dma_fused([xfer(H[a], dm[a], S.farr, T.D[:, CAP * pairs[a][0]:CAP * pairs[a][0] + 2 * CAP], T.F[:, :])
+                        for a in range(4)], local_sem=S.lsem)
+    nt = send(twin, S.rarr1, T.D[:, CAP * kd:CAP * kd + CAP], T.R[:, CAP:2 * CAP])
+    g.remote_dma_fused([xfer(H[1], wm[0], S.warr, T.W[:, :], T.W[:, :]),
+                        xfer(H[3], wm[1], S.warr, T.W[:, :], T.W[:, :])], local_sem=S.lsem)
+
+    g.tensor.wait_ge(S.wl, 32)
+    g.tensor.wait_ge(S.vs, c_d)
+    mm1(0, T.D[:, 0:CAP])
+    relu(0)
+    mm2(0)
+    c_own = out_v(0, T.Z[:, 0:CAP])
+    g.tensor.wait_ge(S.rarr1, nt)
+    mm1(1, T.R[:, CAP:2 * CAP])
+    relu(1)
+    mm2(1)
+    c_tw = out_s(1, T.Yo[:, CAP:2 * CAP])
+    g.wait_ge(S.ss, c_tw)
+    send(cores[(r - kd) % n], S.zarr, T.Yo[:, CAP:2 * CAP], T.Z[:, CAP * kd:CAP * kd + CAP])
+
+    nz = sum(len(_bits(topo.mask(helpers[(r + k) % n][a], core))) for a in range(4) for k in pairs[a])
+    nz += len(_bits(topo.mask(twin, core)))
+    h = TOK // 2
+    ve.wait_ge(S.zarr, nz)
+    c_y = V(lambda: ve.tensor_copy(T.Yf[:, 0:h], T.Z[:, 0:SLOTS + 8].indirect(T.off2[:, 0:16])))
+    g.sync.wait_ge(S.vs, c_y)
+    g.sync.dma_start(T.y[:, 0:h], T.Yf[:, 0:h]).then_inc(S.st, 16)
+    g.scalar.wait_ge(S.zarr, nz)
+    g.scalar.wait_ge(S.vs, c_own)
+    s_y = A(lambda: g.scalar.activation(T.Yf[:, h:TOK], T.Z[:, 0:SLOTS + 8].indirect(T.off2[:, 16:32]),
+                                        ActivationFunctionType.Copy))
+    g.scalar.wait_ge(S.ss, s_y)
+    g.scalar.dma_start(T.y[:, h:TOK], T.Yf[:, h:TOK]).then_inc(S.st, 16)
+    finish([(S.st, 32)])

@@ -49,7 +49,8 @@ SCRATCH = {
 for _b in range(8):
     SCRATCH["B%d" % _b] = ("psum", [128, 512], "float32")
 
-SEMAPHORES = ["vs", "ps", "ss", "gs", "exl", "xl", "wl", "st", "lsem", "farr", "warr", "rarr0", "rarr1", "zarr"]
+SEMAPHORES = ["vs", "ps", "ss", "gs", "exl", "xl", "wl1", "wl2", "st", "lsem", "farr", "warr", "warx", "rarr0", "rarr1",
+              "zarr"]
 
 _PLAN = {}
 
@@ -73,6 +74,7 @@ def _plan(T, topo):
     for c in cores:
         hs = [h for h in range(NSIM) if h != c and topo.host(h) == topo.host(c) and topo.chip(h) == topo.chip(c)
               and all(topo.may_write(h, d) for d in cores)]
+        hs.sort(key=lambda h: (topo.die(h) != topo.die(c), h))
         helpers.append(hs[:4])
     kd = [k for k in range(1, n, 2) if all(topo.may_write(cores[r], cores[(r + k) % n]) for r in range(n))][0]
     rest = [k for k in range(1, n) if k != kd]
@@ -93,6 +95,7 @@ def rank_program(g, core, T, topo):
         return
     S = T.sem
     Op = AluOpType
+    Fn = ActivationFunctionType
     cnt = {"v": 0, "p": 0, "s": 0, "g": 0, "l": 0}
 
     def V(fn):
@@ -128,9 +131,10 @@ def rank_program(g, core, T, topo):
         cnt["l"] += len(_bits(mask))
         return RemoteDMATransfer(dst_ids=[DstId(rid=rid, pnc=pid)], dma_engine_mask=mask, remote_sem=sem, src=src, dst=dst)
 
-    def send(dst_core, sem, src, dst):
+    def send(dst_core, sem, src, dst, mask=None):
         rid, pid = topo.addr(dst_core, core)
-        mask = topo.mask(core, dst_core)
+        if mask is None:
+            mask = topo.mask(core, dst_core)
         cnt["l"] += len(_bits(mask))
         g.remote_dma(out_ap=dst, in_ap=src, remote_sem=sem, local_sem=S.lsem, pid=pid, routing_id=rid,
                      dma_engine_mask=mask)
@@ -153,8 +157,7 @@ def rank_program(g, core, T, topo):
         g.vector.wait_ge(S.ps, st[b]["x"])
         st[b]["hv"] = V(lambda: g.vector.tensor_scalar(T.Hh[:, o:o + 2 * CAP], X[:, 0:2 * CAP], 0.0, None, Op.max))
         g.scalar.wait_ge(S.ps, st[b]["y"])
-        st[b]["hs"] = A(lambda: g.scalar.activation(T.Hh[:, o + 2 * CAP:o + 4 * CAP], Y[:, 0:2 * CAP],
-                                                    ActivationFunctionType.Relu))
+        st[b]["hs"] = A(lambda: g.scalar.activation(T.Hh[:, o + 2 * CAP:o + 4 * CAP], Y[:, 0:2 * CAP], Fn.Relu))
 
     def mm2(b):
         Zb = BK[b][2]
@@ -173,7 +176,7 @@ def rank_program(g, core, T, topo):
 
     def out_s(b, dst):
         g.scalar.wait_ge(S.ps, st[b]["z"])
-        return A(lambda: g.scalar.activation(dst, BK[b][2][:, 0:CAP], ActivationFunctionType.Copy))
+        return A(lambda: g.scalar.activation(dst, BK[b][2][:, 0:CAP], Fn.Copy))
 
     def finish(extra):
         for sem, val in extra + [(S.lsem, cnt["l"]), (S.vs, cnt["v"]), (S.ps, cnt["p"]), (S.ss, cnt["s"]),
@@ -187,16 +190,23 @@ def rank_program(g, core, T, topo):
         d0, d1 = helpers[(r + k0) % n][a], helpers[(r + k1) % n][a]
         m0, m1 = _split(topo.mask(core, d0) & topo.mask(core, d1), 2)
         nf = len(_bits(_split(topo.mask(cores[r], core), 4)[a]))
+        nw = len(_bits(_split(topo.mask(cores[r], core), 2)[0]))
+        nb = helpers[r][a + 1 - 2 * (a % 2)]
+        lo = 512 * (a % 2)
+        g.wait_ge(S.warr, nw)
+        nx = send(nb, S.warx, T.W[:, lo:lo + 512], T.W[:, lo:lo + 512], topo.mask(core, nb) & topo.mask(core, d0))
         g.wait_ge(S.farr, nf)
         g.remote_dma_fused([xfer(d0, m0, S.rarr0, T.F[:, 0:CAP], T.R[:, 0:CAP]),
                             xfer(d1, m1, S.rarr1, T.F[:, CAP:2 * CAP], T.R[:, CAP:2 * CAP])], local_sem=S.lsem)
-        g.tensor.wait_ge(S.warr, len(_bits(_split(topo.mask(cores[r], core), 2)[0])))
+        lay = [(S.warr, nw), (S.warx, nx)]
+        g.tensor.wait_ge(*lay[a % 2])
         g.tensor.wait_ge(S.rarr0, len(_bits(m0)))
         mm1(0, T.R[:, 0:CAP])
         g.tensor.wait_ge(S.rarr1, len(_bits(m1)))
         mm1(1, T.R[:, CAP:2 * CAP])
         relu(0)
         relu(1)
+        g.tensor.wait_ge(*lay[1 - a % 2])
         mm2(0)
         mm2(1)
         c0 = out_v(0, T.Yo[:, 0:CAP])
@@ -211,10 +221,11 @@ def rank_program(g, core, T, topo):
     r = rank
     H = helpers[r]
     ve = g.vector
+    sc = g.scalar
     g.sync.dma_start(T.E16[0:16, :], T.ex[:, :]).then_inc(S.exl, 16)
-    g.scalar.dma_start(T.X[:, :], T.x[:, :]).then_inc(S.xl, 16)
-    g.sync.dma_start(T.W[:, 0:512], T.w1[:, :]).then_inc(S.wl, 16)
-    g.scalar.dma_start(T.W[:, 512:1024], T.w2[:, :]).then_inc(S.wl, 16)
+    sc.dma_start(T.W[:, 0:512], T.w1[:, :]).then_inc(S.wl1, 16)
+    g.sync.dma_start(T.X[:, :], T.x[:, :]).then_inc(S.xl, 16)
+    sc.dma_start(T.W[:, 512:1024], T.w2[:, :]).then_inc(S.wl2, 16)
 
     i_p = G(lambda: g.iota(T.pI[:, :], [[0, 1]], 0, 1))
     i_f = G(lambda: g.iota(T.pF[:, :], [[0, 1]], 0, 1, allow_small_or_imprecise_dtypes=True))
@@ -222,44 +233,48 @@ def rank_program(g, core, T, topo):
     i_cg = G(lambda: g.iota(T.colg[:, :], [[1, 8], [0, 16]], 0, 0, allow_small_or_imprecise_dtypes=True))
     i_t8 = G(lambda: g.iota(T.T8a[:, :], [[16, 32]], SLOTS, 0, allow_small_or_imprecise_dtypes=True))
 
-    V(lambda: ve.memset(T.D[:, 0:SLOTS], 0.0))
     V(lambda: ve.memset(T.MSK[:, :], 1.0))
     V(lambda: ve.memset(T.MSK[:, 32:33], 0.0))
-    V(lambda: ve.memset(T.Z[:, SLOTS:SLOTS + 8], 0.0))
     ve.wait_ge(S.gs, i_p)
     V(lambda: ve.tensor_scalar(T.gI[:, :], T.pI[:, :], 4, None, Op.arith_shift_right))
     V(lambda: ve.tensor_copy(T.eid[:, 0:1], T.gI[:, :]))
-    V(lambda: ve.tensor_scalar(T.eid[:, 1:2], T.eid[:, 0:1], 8.0, None, Op.add))
+    c_e = V(lambda: ve.tensor_scalar(T.eid[:, 1:2], T.eid[:, 0:1], 8.0, None, Op.add))
+    sc.wait_ge(S.vs, c_e)
+    s_b = A(lambda: sc.activation(T.bcb[:, :], T.eid[:, :], Fn.Identity, bias=float(-CAP * r), scale=float(CAP)))
     ve.wait_ge(S.gs, i_f)
-    V(lambda: ve.tensor_scalar(T.rowi[:, :], T.eid[:, 0:1], -16.0, T.pF[:, 0:1], Op.mult, Op.add))
+    c_r = V(lambda: ve.tensor_scalar(T.rowi[:, :], T.eid[:, 0:1], -16.0, T.pF[:, 0:1], Op.mult, Op.add))
+    V(lambda: ve.tensor_scalar(T.bca[:, :], T.eid[:, :], float(r), float(SLOTS), Op.is_lt, Op.mult))
+    ve.wait_ge(S.ss, s_b)
+    V(lambda: ve.tensor_tensor(T.bc[:, :], T.bca[:, :], T.bcb[:, :], Op.add))
     ve.wait_ge(S.gs, i_ci)
     c_sel = V(lambda: ve.tensor_scalar(T.SEL[:, :], T.coli[:, :], T.rowi[:, 0:1], None, Op.is_equal))
+    sc.wait_ge(S.vs, c_sel)
+    A(lambda: sc.activation(T.SB0[:, :], T.SEL[:, :], Fn.Identity, scale=T.bc[:, 0:1]))
+    A(lambda: sc.activation(T.SB1[:, :], T.SEL[:, :], Fn.Identity, scale=T.bc[:, 1:2]))
+    sc.wait_ge(S.gs, i_t8)
+    s_c = A(lambda: sc.activation(T.T8[:, :], T.T8a[:, :], Fn.Identity, bias=T.rowi[:, 0:1]))
+    V(lambda: ve.tensor_scalar(T.LE[:, :], T.coli[:, :], T.rowi[:, 0:1], -1.0, Op.is_le, Op.mult))
     ve.wait_ge(S.gs, i_cg)
     V(lambda: ve.tensor_scalar(T.ON[:, :], T.colg[:, :], T.eid[:, 0:1], None, Op.is_equal))
-    V(lambda: ve.tensor_scalar(T.LE[:, :], T.coli[:, :], T.rowi[:, 0:1], -1.0, Op.is_le, Op.mult))
     V(lambda: ve.tensor_tensor(T.M2[:, :], T.LE[:, :], T.ON[:, :], Op.mult))
-    V(lambda: ve.tensor_scalar(T.bca[:, :], T.eid[:, :], float(r), float(SLOTS), Op.is_lt, Op.mult))
-    V(lambda: ve.tensor_scalar(T.bcb[:, :], T.eid[:, :], float(CAP), float(-CAP * r), Op.mult, Op.add))
-    V(lambda: ve.tensor_tensor(T.bc[:, :], T.bca[:, :], T.bcb[:, :], Op.add))
-    V(lambda: ve.tensor_scalar(T.SB0[:, :], T.SEL[:, :], T.bc[:, 0:1], None, Op.mult))
-    V(lambda: ve.tensor_scalar(T.SB1[:, :], T.SEL[:, :], T.bc[:, 1:2], None, Op.mult))
-    ve.wait_ge(S.gs, i_t8)
-    V(lambda: ve.tensor_scalar(T.T8[:, :], T.T8a[:, :], T.rowi[:, 0:1], None, Op.add))
 
     ve.wait_ge(S.exl, 16)
     c = V(lambda: ve.tensor_copy(T.Ebf[0:16, :], T.E16[0:16, :]))
     g.tensor.wait_ge(S.vs, c)
     p = P(lambda: mm(T.B0[:, 0:32], T.SEL[0:16, :], T.Ebf[0:16, :], True, True))
+    V(lambda: ve.memset(T.D[:, 0:272], 0.0))
     ve.wait_ge(S.ps, p)
     V(lambda: ve.tensor_scalar(T.O[:, 0:32], T.B0[:, 0:32], T.eid[:, 0:1], None, Op.is_equal))
     c_o = V(lambda: ve.tensor_scalar(T.O[:, 32:64], T.B0[:, 0:32], T.eid[:, 1:2], None, Op.is_equal))
     c_s = V(lambda: ve.tensor_tensor_scan(T.Sc[:, :], T.MSK[:, :], T.O[:, :], 0.0, Op.mult, Op.add))
     g.tensor.wait_ge(S.vs, c_o)
+    g.tensor.wait_ge(S.ss, s_c)
     mm(T.B1[:, 0:64], T.M2[:, :], T.O[:, :], True, False)
     mm(T.B2[:, 0:32], T.SB0[:, :], T.O[:, 0:32], True, False)
     mm(T.B2[:, 0:32], T.SB1[:, :], T.O[:, 32:64], False, False)
     g.tensor.wait_ge(S.vs, c_s)
     p = P(lambda: mm(T.B1[:, 0:64], T.ON[:, :], T.Sc[:, :], False, True))
+    V(lambda: ve.memset(T.D[:, 272:544], 0.0))
     ve.wait_ge(S.ps, p)
     c_1 = V(lambda: ve.tensor_tensor(T.R1[:, :], T.B1[:, 0:64], T.O[:, :], Op.mult))
     c_2 = V(lambda: ve.tensor_scalar(T.R2[:, :], T.R1[:, :], float(CAP), 4096.0, Op.is_ge, Op.mult))
@@ -269,27 +284,32 @@ def rank_program(g, core, T, topo):
     g.tensor.wait_ge(S.vs, c_2)
     mm(T.B2[:, 0:32], T.SEL[:, :], T.R2[:, 0:32], False, False)
     p = P(lambda: mm(T.B2[:, 0:32], T.SEL[:, :], T.R2[:, 32:64], False, True))
+    V(lambda: ve.memset(T.D[:, 544:SLOTS], 0.0))
     ve.wait_ge(S.ps, p)
+    ve.wait_ge(S.ss, s_c)
     V(lambda: ve.tensor_tensor(T.OF[:, :], T.B2[:, 0:32], T.T8[:, :], Op.min))
     V(lambda: ve.tensor_copy(T.off1[:, :], T.OF[:, :]))
     ve.wait_ge(S.xl, 16)
     c_d = V(lambda: ve.tensor_copy(T.D[:, 0:SLOTS + TOK].indirect(T.off1[:, 0:32]), T.X[:, :]))
     V(lambda: ve.tensor_scalar(T.off2[:, :], T.OF[:, :], float(SLOTS), None, Op.min))
+    V(lambda: ve.memset(T.Z[:, SLOTS:SLOTS + 8], 0.0))
 
     twin = cores[(r + kd) % n]
     wm = _split(topo.mask(core, H[0]), 2)
-    g.wait_ge(S.wl, 32)
-    g.remote_dma_fused([xfer(H[0], wm[0], S.warr, T.W[:, :], T.W[:, :]),
-                        xfer(H[2], wm[1], S.warr, T.W[:, :], T.W[:, :])], local_sem=S.lsem)
+    g.wait_ge(S.wl1, 16)
+    g.remote_dma_fused([xfer(H[0], wm[0], S.warr, T.W[:, 0:512], T.W[:, 0:512]),
+                        xfer(H[2], wm[1], S.warr, T.W[:, 0:512], T.W[:, 0:512])], local_sem=S.lsem)
+    g.wait_ge(S.wl2, 16)
+    g.remote_dma_fused([xfer(H[1], wm[0], S.warr, T.W[:, 512:1024], T.W[:, 512:1024]),
+                        xfer(H[3], wm[1], S.warr, T.W[:, 512:1024], T.W[:, 512:1024])], local_sem=S.lsem)
     g.wait_ge(S.vs, c_d)
     dm = _split(topo.mask(core, H[0]), 4)
     g.remote_dma_fused([xfer(H[a], dm[a], S.farr, T.D[:, CAP * pairs[a][0]:CAP * pairs[a][0] + 2 * CAP], T.F[:, :])
                         for a in range(4)], local_sem=S.lsem)
     nt = send(twin, S.rarr1, T.D[:, CAP * kd:CAP * kd + CAP], T.R[:, CAP:2 * CAP])
-    g.remote_dma_fused([xfer(H[1], wm[0], S.warr, T.W[:, :], T.W[:, :]),
-                        xfer(H[3], wm[1], S.warr, T.W[:, :], T.W[:, :])], local_sem=S.lsem)
 
-    g.tensor.wait_ge(S.wl, 32)
+    g.tensor.wait_ge(S.wl1, 16)
+    g.tensor.wait_ge(S.wl2, 16)
     g.tensor.wait_ge(S.vs, c_d)
     mm1(0, T.D[:, 0:CAP])
     relu(0)
@@ -308,12 +328,10 @@ def rank_program(g, core, T, topo):
     h = TOK // 2
     ve.wait_ge(S.zarr, nz)
     c_y = V(lambda: ve.tensor_copy(T.Yf[:, 0:h], T.Z[:, 0:SLOTS + 8].indirect(T.off2[:, 0:16])))
+    sc.wait_ge(S.zarr, nz)
+    sc.wait_ge(S.vs, c_own)
+    s_y = A(lambda: sc.activation(T.Yf[:, h:TOK], T.Z[:, 0:SLOTS + 8].indirect(T.off2[:, 16:32]), Fn.Copy))
     g.sync.wait_ge(S.vs, c_y)
-    g.sync.dma_start(T.y[:, 0:h], T.Yf[:, 0:h]).then_inc(S.st, 16)
-    g.scalar.wait_ge(S.zarr, nz)
-    g.scalar.wait_ge(S.vs, c_own)
-    s_y = A(lambda: g.scalar.activation(T.Yf[:, h:TOK], T.Z[:, 0:SLOTS + 8].indirect(T.off2[:, 16:32]),
-                                        ActivationFunctionType.Copy))
-    g.scalar.wait_ge(S.ss, s_y)
-    g.scalar.dma_start(T.y[:, h:TOK], T.Yf[:, h:TOK]).then_inc(S.st, 16)
-    finish([(S.st, 32)])
+    g.sync.wait_ge(S.ss, s_y)
+    g.sync.dma_start(T.y[:, :], T.Yf[:, :]).then_inc(S.st, 16)
+    finish([(S.st, 16)])

@@ -6,11 +6,13 @@ NSIM = 256
 TOK, CAP, FF = 512, 80, 4
 NR = 10
 SLOTS = NR * CAP
+DW = SLOTS + 128 + 16 * 31
+NQ = 48
 
 SCRATCH = {
     "X": ("sbuf", [128, TOK], "bfloat16"),
     "W": ("sbuf", [128, 2 * FF * 128], "bfloat16"),
-    "D": ("sbuf", [128, SLOTS + TOK], "bfloat16"),
+    "D": ("sbuf", [128, DW], "bfloat16"),
     "F": ("sbuf", [128, 2 * CAP], "bfloat16"),
     "R": ("sbuf", [128, 2 * CAP], "bfloat16"),
     "Hh": ("sbuf", [128, 2 * FF * CAP], "bfloat16"),
@@ -19,23 +21,18 @@ SCRATCH = {
     "Yf": ("sbuf", [128, TOK], "bfloat16"),
     "E16": ("sbuf", [128, 32], "int32"),
     "Ebf": ("sbuf", [128, 32], "bfloat16"),
-    "pI": ("sbuf", [128, 1], "int32"),
-    "gI": ("sbuf", [128, 1], "int32"),
-    "pF": ("sbuf", [128, 1], "float32"),
-    "eid": ("sbuf", [128, 2], "float32"),
-    "rowi": ("sbuf", [128, 1], "float32"),
-    "bca": ("sbuf", [128, 2], "float32"),
-    "bcb": ("sbuf", [128, 2], "float32"),
-    "bc": ("sbuf", [128, 2], "float32"),
-    "coli": ("sbuf", [128, 128], "bfloat16"),
-    "colg": ("sbuf", [128, 128], "bfloat16"),
+    "b1": ("sbuf", [128, 32], "bfloat16"),
+    "b2": ("sbuf", [128, 32], "bfloat16"),
+    "Qs": ("sbuf", [128, 128], "int32"),
+    "q15": ("sbuf", [128, 128], "int32"),
+    "Dg": ("sbuf", [128, 128], "int32"),
+    "dsh": ("sbuf", [128, 128], "int32"),
+    "EI": ("sbuf", [128, 64], "int32"),
+    "EIDT": ("sbuf", [128, 64], "int32"),
     "SEL": ("sbuf", [128, 128], "bfloat16"),
     "ON": ("sbuf", [128, 128], "bfloat16"),
-    "LE": ("sbuf", [128, 128], "bfloat16"),
+    "Bn": ("sbuf", [128, 128], "bfloat16"),
     "M2": ("sbuf", [128, 128], "bfloat16"),
-    "SB0": ("sbuf", [128, 128], "bfloat16"),
-    "SB1": ("sbuf", [128, 128], "bfloat16"),
-    "T8a": ("sbuf", [128, 32], "float32"),
     "T8": ("sbuf", [128, 32], "float32"),
     "MSK": ("sbuf", [128, 64], "bfloat16"),
     "O": ("sbuf", [128, 64], "bfloat16"),
@@ -49,8 +46,8 @@ SCRATCH = {
 for _b in range(8):
     SCRATCH["B%d" % _b] = ("psum", [128, 512], "float32")
 
-SEMAPHORES = ["vs", "ps", "ss", "gs", "exl", "xl", "wl1", "wl2", "st", "lsem", "farr", "warr", "warx", "rarr0", "rarr1",
-              "zarr"]
+SEMAPHORES = ["mk", "exl", "xl", "wl1", "wl2", "st", "lsem", "farr", "warr", "warx", "rarr0", "rarr1", "zarr"] + \
+             ["q%d" % _i for _i in range(NQ)]
 
 _PLAN = {}
 
@@ -96,35 +93,18 @@ def rank_program(g, core, T, topo):
     S = T.sem
     Op = AluOpType
     Fn = ActivationFunctionType
-    cnt = {"v": 0, "p": 0, "s": 0, "g": 0, "l": 0}
+    ve, sc, pe = g.vector, g.scalar, g.tensor
+    cnt = {"q": 0, "l": 0}
 
-    def V(fn):
-        if cnt["v"]:
-            g.vector.wait_ge(S.vs, cnt["v"])
-        fn().then_inc(S.vs, 1)
-        cnt["v"] += 1
-        return cnt["v"]
+    def sig(ins):
+        s = S["q%d" % cnt["q"]]
+        cnt["q"] += 1
+        ins.then_inc(s, 1)
+        return s
 
-    def P(fn):
-        if cnt["p"]:
-            g.tensor.wait_ge(S.ps, cnt["p"])
-        fn().then_inc(S.ps, 1)
-        cnt["p"] += 1
-        return cnt["p"]
-
-    def A(fn):
-        if cnt["s"]:
-            g.scalar.wait_ge(S.ss, cnt["s"])
-        fn().then_inc(S.ss, 1)
-        cnt["s"] += 1
-        return cnt["s"]
-
-    def G(fn):
-        if cnt["g"]:
-            g.wait_ge(S.gs, cnt["g"])
-        fn().then_inc(S.gs, 1)
-        cnt["g"] += 1
-        return cnt["g"]
+    def need(q, *sems):
+        for s in sems:
+            q.wait_ge(s, 1)
 
     def xfer(dst_core, mask, sem, src, dst):
         rid, pid = topo.addr(dst_core, core)
@@ -140,49 +120,42 @@ def rank_program(g, core, T, topo):
                      dma_engine_mask=mask)
         return len(_bits(mask))
 
-    mm = g.tensor.matmul
+    mm = pe.matmul
     BK = [(T.B3, T.B4, T.B5), (T.B6, T.B7, T.B0)]
     st = [{}, {}]
 
     def mm1(b, rhs):
         X, Y, _ = BK[b]
         mm(X[:, 0:CAP], T.W[:, 0:128], rhs, True, True)
-        st[b]["x"] = P(lambda: mm(X[:, CAP:2 * CAP], T.W[:, 128:256], rhs, True, True))
+        st[b]["x"] = sig(mm(X[:, CAP:2 * CAP], T.W[:, 128:256], rhs, True, True))
         mm(Y[:, 0:CAP], T.W[:, 256:384], rhs, True, True)
-        st[b]["y"] = P(lambda: mm(Y[:, CAP:2 * CAP], T.W[:, 384:512], rhs, True, True))
+        st[b]["y"] = sig(mm(Y[:, CAP:2 * CAP], T.W[:, 384:512], rhs, True, True))
 
     def relu(b):
         X, Y, _ = BK[b]
         o = b * FF * CAP
-        g.vector.wait_ge(S.ps, st[b]["x"])
-        st[b]["hv"] = V(lambda: g.vector.tensor_scalar(T.Hh[:, o:o + 2 * CAP], X[:, 0:2 * CAP], 0.0, None, Op.max))
-        g.scalar.wait_ge(S.ps, st[b]["y"])
-        st[b]["hs"] = A(lambda: g.scalar.activation(T.Hh[:, o + 2 * CAP:o + 4 * CAP], Y[:, 0:2 * CAP], Fn.Relu))
+        need(ve, st[b]["x"])
+        st[b]["hv"] = sig(ve.tensor_scalar(T.Hh[:, o:o + 2 * CAP], X[:, 0:2 * CAP], 0.0, None, Op.max))
+        need(sc, st[b]["y"])
+        st[b]["hs"] = sig(sc.activation(T.Hh[:, o + 2 * CAP:o + 4 * CAP], Y[:, 0:2 * CAP], Fn.Relu))
 
     def mm2(b):
         Zb = BK[b][2]
         o = b * FF * CAP
-        g.tensor.wait_ge(S.vs, st[b]["hv"])
-        g.tensor.wait_ge(S.ss, st[b]["hs"])
+        need(pe, st[b]["hv"], st[b]["hs"])
         for f in range(FF - 1):
             mm(Zb[:, 0:CAP], T.W[:, 512 + 128 * f:640 + 128 * f], T.Hh[:, o + CAP * f:o + CAP * f + CAP], f == 0, False)
         f = FF - 1
-        st[b]["z"] = P(lambda: mm(Zb[:, 0:CAP], T.W[:, 512 + 128 * f:640 + 128 * f],
-                                  T.Hh[:, o + CAP * f:o + CAP * f + CAP], False, True))
+        st[b]["z"] = sig(mm(Zb[:, 0:CAP], T.W[:, 512 + 128 * f:640 + 128 * f], T.Hh[:, o + CAP * f:o + CAP * f + CAP],
+                            False, True))
 
     def out_v(b, dst):
-        g.vector.wait_ge(S.ps, st[b]["z"])
-        return V(lambda: g.vector.tensor_copy(dst, BK[b][2][:, 0:CAP]))
+        need(ve, st[b]["z"])
+        return sig(ve.tensor_copy(dst, BK[b][2][:, 0:CAP]))
 
     def out_s(b, dst):
-        g.scalar.wait_ge(S.ps, st[b]["z"])
-        return A(lambda: g.scalar.activation(dst, BK[b][2][:, 0:CAP], Fn.Copy))
-
-    def finish(extra):
-        for sem, val in extra + [(S.lsem, cnt["l"]), (S.vs, cnt["v"]), (S.ps, cnt["p"]), (S.ss, cnt["s"]),
-                                 (S.gs, cnt["g"])]:
-            if val:
-                g.wait_ge(sem, val)
+        need(sc, st[b]["z"])
+        return sig(sc.activation(dst, BK[b][2][:, 0:CAP], Fn.Copy))
 
     if rank is None:
         r, a = role[core]
@@ -199,100 +172,93 @@ def rank_program(g, core, T, topo):
         g.remote_dma_fused([xfer(d0, m0, S.rarr0, T.F[:, 0:CAP], T.R[:, 0:CAP]),
                             xfer(d1, m1, S.rarr1, T.F[:, CAP:2 * CAP], T.R[:, CAP:2 * CAP])], local_sem=S.lsem)
         lay = [(S.warr, nw), (S.warx, nx)]
-        g.tensor.wait_ge(*lay[a % 2])
-        g.tensor.wait_ge(S.rarr0, len(_bits(m0)))
+        pe.wait_ge(*lay[a % 2])
+        pe.wait_ge(S.rarr0, len(_bits(m0)))
         mm1(0, T.R[:, 0:CAP])
-        g.tensor.wait_ge(S.rarr1, len(_bits(m1)))
+        pe.wait_ge(S.rarr1, len(_bits(m1)))
         mm1(1, T.R[:, CAP:2 * CAP])
         relu(0)
         relu(1)
-        g.tensor.wait_ge(*lay[1 - a % 2])
+        pe.wait_ge(*lay[1 - a % 2])
         mm2(0)
         mm2(1)
         c0 = out_v(0, T.Yo[:, 0:CAP])
         c1 = out_s(1, T.Yo[:, CAP:2 * CAP])
-        g.wait_ge(S.vs, c0)
+        need(g, c0)
         send(cores[(r - k0) % n], S.zarr, T.Yo[:, 0:CAP], T.Z[:, CAP * k0:CAP * k0 + CAP])
-        g.wait_ge(S.ss, c1)
+        need(g, c1)
         send(cores[(r - k1) % n], S.zarr, T.Yo[:, CAP:2 * CAP], T.Z[:, CAP * k1:CAP * k1 + CAP])
-        finish([])
+        g.wait_ge(S.lsem, cnt["l"])
         return
 
     r = rank
     H = helpers[r]
-    ve = g.vector
-    sc = g.scalar
     g.sync.dma_start(T.E16[0:16, :], T.ex[:, :]).then_inc(S.exl, 16)
     sc.dma_start(T.W[:, 0:512], T.w1[:, :]).then_inc(S.wl1, 16)
     g.sync.dma_start(T.X[:, :], T.x[:, :]).then_inc(S.xl, 16)
     sc.dma_start(T.W[:, 512:1024], T.w2[:, :]).then_inc(S.wl2, 16)
 
-    i_p = G(lambda: g.iota(T.pI[:, :], [[0, 1]], 0, 1))
-    i_f = G(lambda: g.iota(T.pF[:, :], [[0, 1]], 0, 1, allow_small_or_imprecise_dtypes=True))
-    i_ci = G(lambda: g.iota(T.coli[:, :], [[0, 8], [1, 16]], 0, 0, allow_small_or_imprecise_dtypes=True))
-    i_cg = G(lambda: g.iota(T.colg[:, :], [[1, 8], [0, 16]], 0, 0, allow_small_or_imprecise_dtypes=True))
-    i_t8 = G(lambda: g.iota(T.T8a[:, :], [[16, 32]], SLOTS, 0, allow_small_or_imprecise_dtypes=True))
+    i_q = sig(g.iota(T.Qs[:, :], [[-1, 128]], 128, 1))
+    i_e = sig(g.iota(T.EI[:, :], [[128, 2], [0, 32]], 0, 1))
+    i_d = sig(g.iota(T.Dg[:, :], [[-16, 8], [0, 16]], 0, 1))
+    i_t = sig(g.iota(T.T8[:, :], [[16, 32]], SLOTS, 1, allow_small_or_imprecise_dtypes=True))
 
-    V(lambda: ve.memset(T.MSK[:, :], 1.0))
-    V(lambda: ve.memset(T.MSK[:, 32:33], 0.0))
-    ve.wait_ge(S.gs, i_p)
-    V(lambda: ve.tensor_scalar(T.gI[:, :], T.pI[:, :], 4, None, Op.arith_shift_right))
-    V(lambda: ve.tensor_copy(T.eid[:, 0:1], T.gI[:, :]))
-    c_e = V(lambda: ve.tensor_scalar(T.eid[:, 1:2], T.eid[:, 0:1], 8.0, None, Op.add))
-    sc.wait_ge(S.vs, c_e)
-    s_b = A(lambda: sc.activation(T.bcb[:, :], T.eid[:, :], Fn.Identity, bias=float(-CAP * r), scale=float(CAP)))
-    ve.wait_ge(S.gs, i_f)
-    c_r = V(lambda: ve.tensor_scalar(T.rowi[:, :], T.eid[:, 0:1], -16.0, T.pF[:, 0:1], Op.mult, Op.add))
-    V(lambda: ve.tensor_scalar(T.bca[:, :], T.eid[:, :], float(r), float(SLOTS), Op.is_lt, Op.mult))
-    ve.wait_ge(S.ss, s_b)
-    V(lambda: ve.tensor_tensor(T.bc[:, :], T.bca[:, :], T.bcb[:, :], Op.add))
-    ve.wait_ge(S.gs, i_ci)
-    c_sel = V(lambda: ve.tensor_scalar(T.SEL[:, :], T.coli[:, :], T.rowi[:, 0:1], None, Op.is_equal))
-    sc.wait_ge(S.vs, c_sel)
-    A(lambda: sc.activation(T.SB0[:, :], T.SEL[:, :], Fn.Identity, scale=T.bc[:, 0:1]))
-    A(lambda: sc.activation(T.SB1[:, :], T.SEL[:, :], Fn.Identity, scale=T.bc[:, 1:2]))
-    sc.wait_ge(S.gs, i_t8)
-    s_c = A(lambda: sc.activation(T.T8[:, :], T.T8a[:, :], Fn.Identity, bias=T.rowi[:, 0:1]))
-    V(lambda: ve.tensor_scalar(T.LE[:, :], T.coli[:, :], T.rowi[:, 0:1], -1.0, Op.is_le, Op.mult))
-    ve.wait_ge(S.gs, i_cg)
-    V(lambda: ve.tensor_scalar(T.ON[:, :], T.colg[:, :], T.eid[:, 0:1], None, Op.is_equal))
-    V(lambda: ve.tensor_tensor(T.M2[:, :], T.LE[:, :], T.ON[:, :], Op.mult))
+    c_dm = sig(ve.memset(T.D[:, 0:SLOTS], 0.0))
+    ve.memset(T.MSK[:, 0:32], 1.0).then_inc(S.mk, 1)
+    ve.memset(T.MSK[:, 32:33], 0.0).then_inc(S.mk, 1)
+    ve.memset(T.MSK[:, 33:64], 1.0).then_inc(S.mk, 1)
+    c_zm = sig(ve.memset(T.Z[:, SLOTS:SLOTS + 8], 0.0))
+    need(ve, i_q)
+    c_q = sig(ve.tensor_scalar(T.q15[:, :], T.Qs[:, :], 15, None, Op.bitwise_and))
+    c_bn = sig(ve.tensor_scalar(T.Bn[:, :], T.Qs[:, :], 128.0, -1.0, Op.is_ge, Op.mult))
+    need(ve, c_q)
+    c_sel = sig(ve.tensor_scalar(T.SEL[:, :], T.q15[:, :], 0.0, None, Op.is_equal))
+    need(ve, i_e)
+    c_et = sig(ve.tensor_scalar(T.EIDT[:, :], T.EI[:, :], 4, None, Op.arith_shift_right))
+    need(ve, i_d)
+    c_ds = sig(ve.tensor_scalar(T.dsh[:, :], T.Dg[:, :], 4, None, Op.arith_shift_right))
+    need(ve, c_ds)
+    c_on = sig(ve.tensor_scalar(T.ON[:, :], T.dsh[:, :], 0.0, None, Op.is_equal))
+    need(ve, c_on, c_bn)
+    c_m2 = sig(ve.tensor_tensor(T.M2[:, :], T.ON[:, :], T.Bn[:, :], Op.mult))
 
     ve.wait_ge(S.exl, 16)
-    c = V(lambda: ve.tensor_copy(T.Ebf[0:16, :], T.E16[0:16, :]))
-    g.tensor.wait_ge(S.vs, c)
-    p = P(lambda: mm(T.B0[:, 0:32], T.SEL[0:16, :], T.Ebf[0:16, :], True, True))
-    V(lambda: ve.memset(T.D[:, 0:272], 0.0))
-    ve.wait_ge(S.ps, p)
-    V(lambda: ve.tensor_scalar(T.O[:, 0:32], T.B0[:, 0:32], T.eid[:, 0:1], None, Op.is_equal))
-    c_o = V(lambda: ve.tensor_scalar(T.O[:, 32:64], T.B0[:, 0:32], T.eid[:, 1:2], None, Op.is_equal))
-    c_s = V(lambda: ve.tensor_tensor_scan(T.Sc[:, :], T.MSK[:, :], T.O[:, :], 0.0, Op.mult, Op.add))
-    g.tensor.wait_ge(S.vs, c_o)
-    g.tensor.wait_ge(S.ss, s_c)
+    c_e = sig(ve.tensor_copy(T.Ebf[0:16, :], T.E16[0:16, :]))
+    c_b1 = sig(ve.tensor_scalar(T.b1[0:16, :], T.E16[0:16, :], float(r), float(SLOTS), Op.is_lt, Op.mult))
+    c_b2 = sig(ve.tensor_scalar(T.b2[0:16, :], T.E16[0:16, :], float(CAP), float(-CAP * r), Op.mult, Op.add))
+    need(pe, c_sel, c_e)
+    mm(T.B0[:, 0:32], T.SEL[0:16, :], T.Ebf[0:16, :], True, True)
+    p0 = sig(mm(T.B0[:, 32:64], T.SEL[0:16, :], T.Ebf[0:16, :], True, True))
+    need(pe, c_b1, c_b2)
+    mm(T.B2[:, 0:32], T.SEL[0:16, :], T.b1[0:16, :], True, False)
+    mm(T.B2[:, 0:32], T.SEL[0:16, :], T.b2[0:16, :], False, False)
+    need(ve, p0, c_et)
+    c_o = sig(ve.tensor_tensor(T.O[:, :], T.B0[:, 0:64], T.EIDT[:, :], Op.is_equal))
+    need(ve, c_o)
+    ve.wait_ge(S.mk, 3)
+    c_s = sig(ve.tensor_tensor_scan(T.Sc[:, :], T.MSK[:, :], T.O[:, :], 0.0, Op.mult, Op.add))
+    need(pe, c_o, c_m2)
     mm(T.B1[:, 0:64], T.M2[:, :], T.O[:, :], True, False)
-    mm(T.B2[:, 0:32], T.SB0[:, :], T.O[:, 0:32], True, False)
-    mm(T.B2[:, 0:32], T.SB1[:, :], T.O[:, 32:64], False, False)
-    g.tensor.wait_ge(S.vs, c_s)
-    p = P(lambda: mm(T.B1[:, 0:64], T.ON[:, :], T.Sc[:, :], False, True))
-    V(lambda: ve.memset(T.D[:, 272:544], 0.0))
-    ve.wait_ge(S.ps, p)
-    c_1 = V(lambda: ve.tensor_tensor(T.R1[:, :], T.B1[:, 0:64], T.O[:, :], Op.mult))
-    c_2 = V(lambda: ve.tensor_scalar(T.R2[:, :], T.R1[:, :], float(CAP), 4096.0, Op.is_ge, Op.mult))
-    g.tensor.wait_ge(S.vs, c_1)
+    need(pe, c_s)
+    p1 = sig(mm(T.B1[:, 0:64], T.ON[:, :], T.Sc[:, :], False, True))
+    need(ve, p1)
+    c_1 = sig(ve.tensor_tensor(T.R1[:, :], T.B1[:, 0:64], T.O[:, :], Op.mult))
+    need(ve, c_1)
+    c_2 = sig(ve.tensor_scalar(T.R2[:, :], T.R1[:, :], float(CAP), 4096.0, Op.is_ge, Op.mult))
+    need(pe, c_1)
     mm(T.B2[:, 0:32], T.SEL[:, :], T.R1[:, 0:32], False, False)
     mm(T.B2[:, 0:32], T.SEL[:, :], T.R1[:, 32:64], False, False)
-    g.tensor.wait_ge(S.vs, c_2)
+    need(pe, c_2)
     mm(T.B2[:, 0:32], T.SEL[:, :], T.R2[:, 0:32], False, False)
-    p = P(lambda: mm(T.B2[:, 0:32], T.SEL[:, :], T.R2[:, 32:64], False, True))
-    V(lambda: ve.memset(T.D[:, 544:SLOTS], 0.0))
-    ve.wait_ge(S.ps, p)
-    ve.wait_ge(S.ss, s_c)
-    V(lambda: ve.tensor_tensor(T.OF[:, :], T.B2[:, 0:32], T.T8[:, :], Op.min))
-    V(lambda: ve.tensor_copy(T.off1[:, :], T.OF[:, :]))
+    p2 = sig(mm(T.B2[:, 0:32], T.SEL[:, :], T.R2[:, 32:64], False, True))
+    need(ve, p2, i_t)
+    c_of = sig(ve.tensor_tensor(T.OF[:, :], T.B2[:, 0:32], T.T8[:, :], Op.min))
+    need(ve, c_of)
+    c_f1 = sig(ve.tensor_copy(T.off1[:, :], T.OF[:, :]))
+    need(ve, c_f1, c_dm)
     ve.wait_ge(S.xl, 16)
-    c_d = V(lambda: ve.tensor_copy(T.D[:, 0:SLOTS + TOK].indirect(T.off1[:, 0:32]), T.X[:, :]))
-    V(lambda: ve.tensor_scalar(T.off2[:, :], T.OF[:, :], float(SLOTS), None, Op.min))
-    V(lambda: ve.memset(T.Z[:, SLOTS:SLOTS + 8], 0.0))
+    c_d = sig(ve.tensor_copy(T.D[:, 0:DW].indirect(T.off1[:, 0:32]), T.X[:, :]))
+    c_f2 = sig(ve.tensor_scalar(T.off2[:, :], T.OF[:, :], float(SLOTS), None, Op.min))
 
     twin = cores[(r + kd) % n]
     wm = _split(topo.mask(core, H[0]), 2)
@@ -302,36 +268,37 @@ def rank_program(g, core, T, topo):
     g.wait_ge(S.wl2, 16)
     g.remote_dma_fused([xfer(H[1], wm[0], S.warr, T.W[:, 512:1024], T.W[:, 512:1024]),
                         xfer(H[3], wm[1], S.warr, T.W[:, 512:1024], T.W[:, 512:1024])], local_sem=S.lsem)
-    g.wait_ge(S.vs, c_d)
+    need(g, c_d)
     dm = _split(topo.mask(core, H[0]), 4)
     g.remote_dma_fused([xfer(H[a], dm[a], S.farr, T.D[:, CAP * pairs[a][0]:CAP * pairs[a][0] + 2 * CAP], T.F[:, :])
                         for a in range(4)], local_sem=S.lsem)
     nt = send(twin, S.rarr1, T.D[:, CAP * kd:CAP * kd + CAP], T.R[:, CAP:2 * CAP])
 
-    g.tensor.wait_ge(S.wl1, 16)
-    g.tensor.wait_ge(S.wl2, 16)
-    g.tensor.wait_ge(S.vs, c_d)
+    pe.wait_ge(S.wl1, 16)
+    pe.wait_ge(S.wl2, 16)
+    need(pe, c_d)
     mm1(0, T.D[:, 0:CAP])
     relu(0)
     mm2(0)
     c_own = out_v(0, T.Z[:, 0:CAP])
-    g.tensor.wait_ge(S.rarr1, nt)
+    pe.wait_ge(S.rarr1, nt)
     mm1(1, T.R[:, CAP:2 * CAP])
     relu(1)
     mm2(1)
     c_tw = out_s(1, T.Yo[:, CAP:2 * CAP])
-    g.wait_ge(S.ss, c_tw)
+    need(g, c_tw)
     send(cores[(r - kd) % n], S.zarr, T.Yo[:, CAP:2 * CAP], T.Z[:, CAP * kd:CAP * kd + CAP])
 
     nz = sum(len(_bits(topo.mask(helpers[(r + k) % n][a], core))) for a in range(4) for k in pairs[a])
     nz += len(_bits(topo.mask(twin, core)))
     h = TOK // 2
+    need(ve, c_f2, c_own, c_zm)
     ve.wait_ge(S.zarr, nz)
-    c_y = V(lambda: ve.tensor_copy(T.Yf[:, 0:h], T.Z[:, 0:SLOTS + 8].indirect(T.off2[:, 0:16])))
+    c_y = sig(ve.tensor_copy(T.Yf[:, 0:h], T.Z[:, 0:SLOTS + 8].indirect(T.off2[:, 0:16])))
+    need(sc, c_f2, c_own, c_zm)
     sc.wait_ge(S.zarr, nz)
-    sc.wait_ge(S.vs, c_own)
-    s_y = A(lambda: sc.activation(T.Yf[:, h:TOK], T.Z[:, 0:SLOTS + 8].indirect(T.off2[:, 16:32]), Fn.Copy))
-    g.sync.wait_ge(S.vs, c_y)
-    g.sync.wait_ge(S.ss, s_y)
+    s_y = sig(sc.activation(T.Yf[:, h:TOK], T.Z[:, 0:SLOTS + 8].indirect(T.off2[:, 16:32]), Fn.Copy))
+    need(g.sync, c_y, s_y)
     g.sync.dma_start(T.y[:, :], T.Yf[:, :]).then_inc(S.st, 16)
-    finish([(S.st, 16)])
+    g.wait_ge(S.st, 16)
+    g.wait_ge(S.lsem, cnt["l"])

@@ -25,14 +25,15 @@ SCRATCH = {
     "b2": ("sbuf", [128, 32], "bfloat16"),
     "Qs": ("sbuf", [128, 128], "int32"),
     "q15": ("sbuf", [128, 128], "int32"),
-    "Dg": ("sbuf", [128, 128], "int32"),
-    "dsh": ("sbuf", [128, 128], "int32"),
+    "Dg": ("sbuf", [128, 128], "bfloat16"),
     "EI": ("sbuf", [128, 64], "int32"),
     "EIDT": ("sbuf", [128, 64], "int32"),
     "SEL": ("sbuf", [128, 128], "bfloat16"),
-    "ON": ("sbuf", [128, 128], "bfloat16"),
     "Bn": ("sbuf", [128, 128], "bfloat16"),
-    "M2": ("sbuf", [128, 128], "bfloat16"),
+    "I1k": ("sbuf", [128, 128], "bfloat16"),
+    "G0": ("sbuf", [128, 128], "bfloat16"),
+    "G16": ("sbuf", [128, 128], "bfloat16"),
+    "G16n": ("sbuf", [128, 128], "bfloat16"),
     "T8": ("sbuf", [128, 32], "float32"),
     "MSK": ("sbuf", [128, 64], "bfloat16"),
     "O": ("sbuf", [128, 64], "bfloat16"),
@@ -46,7 +47,7 @@ SCRATCH = {
 for _b in range(8):
     SCRATCH["B%d" % _b] = ("psum", [128, 512], "float32")
 
-SEMAPHORES = ["mk", "exl", "xl", "wl1", "wl2", "st", "lsem", "farr", "warr", "warx", "rarr0", "rarr1", "zarr"] + \
+SEMAPHORES = ["mk", "exl", "xl", "wl1", "wl2", "st", "lsem", "farr", "warr", "warx", "wars", "rarr0", "rarr1", "zarr"] + \
              ["q%d" % _i for _i in range(NQ)]
 
 _PLAN = {}
@@ -162,24 +163,23 @@ def rank_program(g, core, T, topo):
         k0, k1 = pairs[a]
         d0, d1 = helpers[(r + k0) % n][a], helpers[(r + k1) % n][a]
         m0, m1 = _split(topo.mask(core, d0) & topo.mask(core, d1), 2)
-        nf = len(_bits(_split(topo.mask(cores[r], core), 4)[a]))
-        nw = len(_bits(_split(topo.mask(cores[r], core), 2)[0]))
+        nq = len(_bits(_split(topo.mask(cores[r], core), 4)[a]))
         nb = helpers[r][a + 1 - 2 * (a % 2)]
-        lo = 512 * (a % 2)
-        g.wait_ge(S.warr, nw)
-        nx = send(nb, S.warx, T.W[:, lo:lo + 512], T.W[:, lo:lo + 512], topo.mask(core, nb) & topo.mask(core, d0))
-        g.wait_ge(S.farr, nf)
+        lo = 256 * (a % 2)
+        g.wait_ge(S.warr, nq)
+        nx = send(nb, S.warx, T.W[:, lo:lo + 256], T.W[:, lo:lo + 256], topo.mask(core, nb) & topo.mask(core, d0))
+        g.wait_ge(S.farr, nq)
         g.remote_dma_fused([xfer(d0, m0, S.rarr0, T.F[:, 0:CAP], T.R[:, 0:CAP]),
                             xfer(d1, m1, S.rarr1, T.F[:, CAP:2 * CAP], T.R[:, CAP:2 * CAP])], local_sem=S.lsem)
-        lay = [(S.warr, nw), (S.warx, nx)]
-        pe.wait_ge(*lay[a % 2])
+        pe.wait_ge(S.warr, nq)
+        pe.wait_ge(S.warx, nx)
         pe.wait_ge(S.rarr0, len(_bits(m0)))
         mm1(0, T.R[:, 0:CAP])
         pe.wait_ge(S.rarr1, len(_bits(m1)))
         mm1(1, T.R[:, CAP:2 * CAP])
         relu(0)
         relu(1)
-        pe.wait_ge(*lay[1 - a % 2])
+        pe.wait_ge(S.wars, nq)
         mm2(0)
         mm2(1)
         c0 = out_v(0, T.Yo[:, 0:CAP])
@@ -200,7 +200,7 @@ def rank_program(g, core, T, topo):
 
     i_q = sig(g.iota(T.Qs[:, :], [[-1, 128]], 128, 1))
     i_e = sig(g.iota(T.EI[:, :], [[128, 2], [0, 32]], 0, 1))
-    i_d = sig(g.iota(T.Dg[:, :], [[-16, 8], [0, 16]], 0, 1))
+    i_d = sig(g.iota(T.Dg[:, :], [[-16, 8], [0, 16]], 0, 1, allow_small_or_imprecise_dtypes=True))
     i_t = sig(g.iota(T.T8[:, :], [[16, 32]], SLOTS, 1, allow_small_or_imprecise_dtypes=True))
 
     c_dm = sig(ve.memset(T.D[:, 0:SLOTS], 0.0))
@@ -211,16 +211,15 @@ def rank_program(g, core, T, topo):
     need(ve, i_q)
     c_q = sig(ve.tensor_scalar(T.q15[:, :], T.Qs[:, :], 15, None, Op.bitwise_and))
     c_bn = sig(ve.tensor_scalar(T.Bn[:, :], T.Qs[:, :], 128.0, -1.0, Op.is_ge, Op.mult))
+    c_ik = sig(ve.tensor_scalar(T.I1k[:, :], T.Qs[:, :], 128.0, 1024.0, Op.is_equal, Op.mult))
     need(ve, c_q)
     c_sel = sig(ve.tensor_scalar(T.SEL[:, :], T.q15[:, :], 0.0, None, Op.is_equal))
     need(ve, i_e)
     c_et = sig(ve.tensor_scalar(T.EIDT[:, :], T.EI[:, :], 4, None, Op.arith_shift_right))
     need(ve, i_d)
-    c_ds = sig(ve.tensor_scalar(T.dsh[:, :], T.Dg[:, :], 4, None, Op.arith_shift_right))
-    need(ve, c_ds)
-    c_on = sig(ve.tensor_scalar(T.ON[:, :], T.dsh[:, :], 0.0, None, Op.is_equal))
-    need(ve, c_on, c_bn)
-    c_m2 = sig(ve.tensor_tensor(T.M2[:, :], T.ON[:, :], T.Bn[:, :], Op.mult))
+    c_g16 = sig(ve.tensor_scalar(T.G16[:, :], T.Dg[:, :], 16.0, None, Op.is_ge))
+    c_g0 = sig(ve.tensor_scalar(T.G0[:, :], T.Dg[:, :], 0.0, None, Op.is_ge))
+    c_g16n = sig(ve.tensor_scalar(T.G16n[:, :], T.Dg[:, :], 16.0, -1.0, Op.is_ge, Op.mult))
 
     ve.wait_ge(S.exl, 16)
     c_e = sig(ve.tensor_copy(T.Ebf[0:16, :], T.E16[0:16, :]))
@@ -237,14 +236,16 @@ def rank_program(g, core, T, topo):
     need(ve, c_o)
     ve.wait_ge(S.mk, 3)
     c_s = sig(ve.tensor_tensor_scan(T.Sc[:, :], T.MSK[:, :], T.O[:, :], 0.0, Op.mult, Op.add))
-    need(pe, c_o, c_m2)
-    mm(T.B1[:, 0:64], T.M2[:, :], T.O[:, :], True, False)
-    need(pe, c_s)
-    p1 = sig(mm(T.B1[:, 0:64], T.ON[:, :], T.Sc[:, :], False, True))
+    need(pe, c_o, c_bn, c_ik, c_g16)
+    mm(T.B1[:, 0:64], T.Bn[:, :], T.O[:, :], True, False)
+    mm(T.B1[:, 0:64], T.G16[:, :], T.O[:, :], False, False)
+    mm(T.B1[:, 0:64], T.I1k[:, :], T.O[:, :], False, False)
+    need(pe, c_s, c_g0, c_g16n)
+    mm(T.B1[:, 0:64], T.G0[:, :], T.Sc[:, :], False, False)
+    p1 = sig(mm(T.B1[:, 0:64], T.G16n[:, :], T.Sc[:, :], False, True))
     need(ve, p1)
-    c_1 = sig(ve.tensor_tensor(T.R1[:, :], T.B1[:, 0:64], T.O[:, :], Op.mult))
-    need(ve, c_1)
-    c_2 = sig(ve.tensor_scalar(T.R2[:, :], T.R1[:, :], float(CAP), 4096.0, Op.is_ge, Op.mult))
+    c_1 = sig(ve.tensor_scalar(T.R1[:, :], T.B1[:, 0:64], 1024.0, 0.0, Op.subtract, Op.max))
+    c_2 = sig(ve.tensor_scalar(T.R2[:, :], T.B1[:, 0:64], float(1024 + CAP), 4096.0, Op.is_ge, Op.mult))
     need(pe, c_1)
     mm(T.B2[:, 0:32], T.SEL[:, :], T.R1[:, 0:32], False, False)
     mm(T.B2[:, 0:32], T.SEL[:, :], T.R1[:, 32:64], False, False)
@@ -261,15 +262,14 @@ def rank_program(g, core, T, topo):
     c_f2 = sig(ve.tensor_scalar(T.off2[:, :], T.OF[:, :], float(SLOTS), None, Op.min))
 
     twin = cores[(r + kd) % n]
-    wm = _split(topo.mask(core, H[0]), 2)
-    g.wait_ge(S.wl1, 16)
-    g.remote_dma_fused([xfer(H[0], wm[0], S.warr, T.W[:, 0:512], T.W[:, 0:512]),
-                        xfer(H[2], wm[1], S.warr, T.W[:, 0:512], T.W[:, 0:512])], local_sem=S.lsem)
-    g.wait_ge(S.wl2, 16)
-    g.remote_dma_fused([xfer(H[1], wm[0], S.warr, T.W[:, 512:1024], T.W[:, 512:1024]),
-                        xfer(H[3], wm[1], S.warr, T.W[:, 512:1024], T.W[:, 512:1024])], local_sem=S.lsem)
-    need(g, c_d)
     dm = _split(topo.mask(core, H[0]), 4)
+    g.wait_ge(S.wl1, 16)
+    g.remote_dma_fused([xfer(H[a], dm[a], S.warr, T.W[:, 256 * (a % 2):256 * (a % 2) + 256],
+                             T.W[:, 256 * (a % 2):256 * (a % 2) + 256]) for a in range(4)], local_sem=S.lsem)
+    g.wait_ge(S.wl2, 16)
+    g.remote_dma_fused([xfer(H[a], dm[a], S.wars, T.W[:, 512:1024], T.W[:, 512:1024]) for a in range(4)],
+                       local_sem=S.lsem)
+    need(g, c_d)
     g.remote_dma_fused([xfer(H[a], dm[a], S.farr, T.D[:, CAP * pairs[a][0]:CAP * pairs[a][0] + 2 * CAP], T.F[:, :])
                         for a in range(4)], local_sem=S.lsem)
     nt = send(twin, S.rarr1, T.D[:, CAP * kd:CAP * kd + CAP], T.R[:, CAP:2 * CAP])

@@ -40,7 +40,6 @@ SCRATCH = {
     "Sc": ("sbuf", [128, 64], "bfloat16"),
     "R1": ("sbuf", [128, 64], "bfloat16"),
     "R2": ("sbuf", [128, 64], "bfloat16"),
-    "OF": ("sbuf", [128, 32], "float32"),
     "off1": ("sbuf", [128, 32], "uint16"),
     "off2": ("sbuf", [128, 32], "uint16"),
 }
@@ -143,8 +142,11 @@ def rank_program(g, core, T, topo):
     def mm2(b):
         Zb = BK[b][2]
         o = b * FF * CAP
-        need(pe, st[b]["hv"], st[b]["hs"])
         for f in range(FF - 1):
+            if f == 0:
+                need(pe, st[b]["hv"])
+            if f == FF // 2:
+                need(pe, st[b]["hs"])
             mm(Zb[:, 0:CAP], T.W[:, 512 + 128 * f:640 + 128 * f], T.Hh[:, o + CAP * f:o + CAP * f + CAP], f == 0, False)
         f = FF - 1
         st[b]["z"] = sig(mm(Zb[:, 0:CAP], T.W[:, 512 + 128 * f:640 + 128 * f], T.Hh[:, o + CAP * f:o + CAP * f + CAP],
@@ -204,38 +206,35 @@ def rank_program(g, core, T, topo):
     i_t = sig(g.iota(T.T8[:, :], [[16, 32]], SLOTS, 1, allow_small_or_imprecise_dtypes=True))
 
     c_dm = sig(ve.memset(T.D[:, 0:SLOTS], 0.0))
-    ve.memset(T.MSK[:, 0:32], 1.0).then_inc(S.mk, 1)
-    ve.memset(T.MSK[:, 32:33], 0.0).then_inc(S.mk, 1)
-    ve.memset(T.MSK[:, 33:64], 1.0).then_inc(S.mk, 1)
-    c_zm = sig(ve.memset(T.Z[:, SLOTS:SLOTS + 8], 0.0))
     need(ve, i_q)
     c_q = sig(ve.tensor_scalar(T.q15[:, :], T.Qs[:, :], 15, None, Op.bitwise_and))
     c_bn = sig(ve.tensor_scalar(T.Bn[:, :], T.Qs[:, :], 128.0, -1.0, Op.is_ge, Op.mult))
-    c_ik = sig(ve.tensor_scalar(T.I1k[:, :], T.Qs[:, :], 128.0, 1024.0, Op.is_equal, Op.mult))
     need(ve, c_q)
     c_sel = sig(ve.tensor_scalar(T.SEL[:, :], T.q15[:, :], 0.0, None, Op.is_equal))
     need(ve, i_e)
     c_et = sig(ve.tensor_scalar(T.EIDT[:, :], T.EI[:, :], 4, None, Op.arith_shift_right))
-    need(ve, i_d)
-    c_g16 = sig(ve.tensor_scalar(T.G16[:, :], T.Dg[:, :], 16.0, None, Op.is_ge))
-    c_g0 = sig(ve.tensor_scalar(T.G0[:, :], T.Dg[:, :], 0.0, None, Op.is_ge))
-    c_g16n = sig(ve.tensor_scalar(T.G16n[:, :], T.Dg[:, :], 16.0, -1.0, Op.is_ge, Op.mult))
 
     ve.wait_ge(S.exl, 16)
     c_e = sig(ve.tensor_copy(T.Ebf[0:16, :], T.E16[0:16, :]))
-    c_b1 = sig(ve.tensor_scalar(T.b1[0:16, :], T.E16[0:16, :], float(r), float(SLOTS), Op.is_lt, Op.mult))
-    c_b2 = sig(ve.tensor_scalar(T.b2[0:16, :], T.E16[0:16, :], float(CAP), float(-CAP * r), Op.mult, Op.add))
     need(pe, c_sel, c_e)
     mm(T.B0[:, 0:32], T.SEL[0:16, :], T.Ebf[0:16, :], True, True)
     p0 = sig(mm(T.B0[:, 32:64], T.SEL[0:16, :], T.Ebf[0:16, :], True, True))
-    need(pe, c_b1, c_b2)
-    mm(T.B2[:, 0:32], T.SEL[0:16, :], T.b1[0:16, :], True, False)
-    mm(T.B2[:, 0:32], T.SEL[0:16, :], T.b2[0:16, :], False, False)
+    ve.memset(T.MSK[:, 0:32], 1.0).then_inc(S.mk, 1)
+    ve.memset(T.MSK[:, 32:33], 0.0).then_inc(S.mk, 1)
+    ve.memset(T.MSK[:, 33:64], 1.0).then_inc(S.mk, 1)
+    c_ik = sig(ve.tensor_scalar(T.I1k[:, :], T.Qs[:, :], 128.0, 1024.0, Op.is_equal, Op.mult))
+    need(ve, i_d)
+    c_g16 = sig(ve.tensor_scalar(T.G16[:, :], T.Dg[:, :], 16.0, None, Op.is_ge))
     need(ve, p0, c_et)
     c_o = sig(ve.tensor_tensor(T.O[:, :], T.B0[:, 0:64], T.EIDT[:, :], Op.is_equal))
+    c_g0 = sig(ve.tensor_scalar(T.G0[:, :], T.Dg[:, :], 0.0, None, Op.is_ge))
+    c_g16n = sig(ve.tensor_scalar(T.G16n[:, :], T.Dg[:, :], 16.0, -1.0, Op.is_ge, Op.mult))
     need(ve, c_o)
     ve.wait_ge(S.mk, 3)
     c_s = sig(ve.tensor_tensor_scan(T.Sc[:, :], T.MSK[:, :], T.O[:, :], 0.0, Op.mult, Op.add))
+    c_b1 = sig(ve.tensor_scalar(T.b1[0:16, :], T.E16[0:16, :], float(r), float(SLOTS), Op.is_lt, Op.mult))
+    c_b2 = sig(ve.tensor_scalar(T.b2[0:16, :], T.E16[0:16, :], float(CAP), float(-CAP * r), Op.mult, Op.add))
+    c_zm = sig(ve.memset(T.Z[:, SLOTS:SLOTS + 8], 0.0))
     need(pe, c_o, c_bn, c_ik, c_g16)
     mm(T.B1[:, 0:64], T.Bn[:, :], T.O[:, :], True, False)
     mm(T.B1[:, 0:64], T.G16[:, :], T.O[:, :], False, False)
@@ -243,6 +242,9 @@ def rank_program(g, core, T, topo):
     need(pe, c_s, c_g0, c_g16n)
     mm(T.B1[:, 0:64], T.G0[:, :], T.Sc[:, :], False, False)
     p1 = sig(mm(T.B1[:, 0:64], T.G16n[:, :], T.Sc[:, :], False, True))
+    need(pe, c_b1, c_b2)
+    mm(T.B2[:, 0:32], T.SEL[0:16, :], T.b1[0:16, :], True, False)
+    mm(T.B2[:, 0:32], T.SEL[0:16, :], T.b2[0:16, :], False, False)
     need(ve, p1)
     c_1 = sig(ve.tensor_scalar(T.R1[:, :], T.B1[:, 0:64], 1024.0, 0.0, Op.subtract, Op.max))
     c_2 = sig(ve.tensor_scalar(T.R2[:, :], T.B1[:, 0:64], float(1024 + CAP), 4096.0, Op.is_ge, Op.mult))
@@ -253,13 +255,11 @@ def rank_program(g, core, T, topo):
     mm(T.B2[:, 0:32], T.SEL[:, :], T.R2[:, 0:32], False, False)
     p2 = sig(mm(T.B2[:, 0:32], T.SEL[:, :], T.R2[:, 32:64], False, True))
     need(ve, p2, i_t)
-    c_of = sig(ve.tensor_tensor(T.OF[:, :], T.B2[:, 0:32], T.T8[:, :], Op.min))
-    need(ve, c_of)
-    c_f1 = sig(ve.tensor_copy(T.off1[:, :], T.OF[:, :]))
+    c_f1 = sig(ve.tensor_tensor(T.off1[:, :], T.B2[:, 0:32], T.T8[:, :], Op.min))
     need(ve, c_f1, c_dm)
     ve.wait_ge(S.xl, 16)
     c_d = sig(ve.tensor_copy(T.D[:, 0:DW].indirect(T.off1[:, 0:32]), T.X[:, :]))
-    c_f2 = sig(ve.tensor_scalar(T.off2[:, :], T.OF[:, :], float(SLOTS), None, Op.min))
+    c_f2 = sig(ve.tensor_scalar(T.off2[:, :], T.off1[:, :], float(SLOTS), None, Op.min))
 
     twin = cores[(r + kd) % n]
     dm = _split(topo.mask(core, H[0]), 4)

import comms_topo
from concourse.bass import DstId, RemoteDMATransfer
from concourse.mybir import AluOpType, ActivationFunctionType

NSIM = 256
TOK, CAP, FF = 512, 80, 4
NR = 10
SLOTS = NR * CAP
DW = SLOTS + 128 + 16 * 31
NQ = 48

SCRATCH = {
    "X": ("sbuf", [128, TOK], "bfloat16"),
    "W": ("sbuf", [128, 2 * FF * 128], "bfloat16"),
    "D": ("sbuf", [128, DW], "bfloat16"),
    "F": ("sbuf", [128, 2 * CAP], "bfloat16"),
    "R": ("sbuf", [128, 2 * CAP], "bfloat16"),
    "Hh": ("sbuf", [128, 2 * FF * CAP], "bfloat16"),
    "Yo": ("sbuf", [128, 2 * CAP], "bfloat16"),
    "Z": ("sbuf", [128, SLOTS + 8], "bfloat16"),
    "Yf": ("sbuf", [128, TOK], "bfloat16"),
    "E16": ("sbuf", [128, 32], "int32"),
    "Ebf": ("sbuf", [128, 32], "bfloat16"),
    "b1": ("sbuf", [128, 32], "bfloat16"),
    "b2": ("sbuf", [128, 32], "bfloat16"),
    "Qs": ("sbuf", [128, 128], "int32"),
    "q15": ("sbuf", [128, 128], "int32"),
    "Dg": ("sbuf", [128, 128], "bfloat16"),
    "EI": ("sbuf", [128, 64], "int32"),
    "EIDT": ("sbuf", [128, 64], "int32"),
    "SEL": ("sbuf", [128, 128], "bfloat16"),
    "Bn": ("sbuf", [128, 128], "bfloat16"),
    "I1k": ("sbuf", [128, 128], "bfloat16"),
    "G0": ("sbuf", [128, 128], "bfloat16"),
    "G16": ("sbuf", [128, 128], "bfloat16"),
    "G16n": ("sbuf", [128, 128], "bfloat16"),
    "T8": ("sbuf", [128, 32], "float32"),
    "MSK": ("sbuf", [128, 64], "bfloat16"),
    "O": ("sbuf", [128, 64], "bfloat16"),
    "Sc": ("sbuf", [128, 64], "bfloat16"),
    "R1": ("sbuf", [128, 64], "bfloat16"),
    "R2": ("sbuf", [128, 64], "bfloat16"),
    "off1": ("sbuf", [128, 32], "uint16"),
    "off2": ("sbuf", [128, 32], "uint16"),
}
for _b in range(8):
    SCRATCH["B%d" % _b] = ("psum", [128, 512], "float32")

SEMAPHORES = ["mk", "exl", "xl", "wl1", "wl2", "st", "lsem", "farr", "warr", "warx", "wars", "rarr0", "rarr1", "zarr"] + \
             ["q%d" % _i for _i in range(NQ)]

_PLAN = {}


def _bits(m):
    return [1 << i for i in range(16) if (m >> i) & 1]


def _split(m, n):
    b = _bits(m)
    w = len(b) // n
    return [sum(b[i * w:(i + 1) * w]) for i in range(n)]


def _plan(T, topo):
    if "p" in _PLAN:
        return _PLAN["p"]
    cores = [int(c) for c in T.cores]
    n = len(cores)
    helpers = []
    for c in cores:
        hs = [h for h in range(NSIM) if h != c and topo.host(h) == topo.host(c) and topo.chip(h) == topo.chip(c)
              and all(topo.may_write(h, d) for d in cores)]
        hs.sort(key=lambda h: (topo.die(h) != topo.die(c), h))
        helpers.append(hs[:4])
    kd = [k for k in range(1, n, 2) if all(topo.may_write(cores[r], cores[(r + k) % n]) for r in range(n))][0]
    rest = [k for k in range(1, n) if k != kd]
    pairs = [(rest[2 * a], rest[2 * a + 1]) for a in range(4)]
    role = {}
    for r in range(n):
        for a, h in enumerate(helpers[r]):
            role[h] = (r, a)
    _PLAN["p"] = (cores, helpers, kd, pairs, role)
    return _PLAN["p"]


def rank_program(g, core, T, topo):
    cores, helpers, kd, pairs, role = _plan(T, topo)
    n = len(cores)
    rank = T.rank_of(core)
    if rank is None and core not in role:
        return
    S = T.sem
    Op = AluOpType
    Fn = ActivationFunctionType
    ve, sc, pe = g.vector, g.scalar, g.tensor
    cnt = {"q": 0, "l": 0}

    def sig(ins):
        s = S["q%d" % cnt["q"]]
        cnt["q"] += 1
        ins.then_inc(s, 1)
        return s

    def need(q, *sems):
        for s in sems:
            q.wait_ge(s, 1)

    def xfer(dst_core, mask, sem, src, dst):
        rid, pid = topo.addr(dst_core, core)
        cnt["l"] += len(_bits(mask))
        return RemoteDMATransfer(dst_ids=[DstId(rid=rid, pnc=pid)], dma_engine_mask=mask, remote_sem=sem, src=src, dst=dst)

    def send(dst_core, sem, src, dst, mask=None):
        rid, pid = topo.addr(dst_core, core)
        if mask is None:
            mask = topo.mask(core, dst_core)
        cnt["l"] += len(_bits(mask))
        g.remote_dma(out_ap=dst, in_ap=src, remote_sem=sem, local_sem=S.lsem, pid=pid, routing_id=rid,
                     dma_engine_mask=mask)
        return len(_bits(mask))

    mm = pe.matmul
    BK = [(T.B3, T.B4, T.B5), (T.B6, T.B7, T.B0)]
    st = [{}, {}]

    def mm1(b, rhs):
        X, Y, _ = BK[b]
        mm(X[:, 0:CAP], T.W[:, 0:128], rhs, True, True)
        st[b]["x"] = sig(mm(X[:, CAP:2 * CAP], T.W[:, 128:256], rhs, True, True))
        mm(Y[:, 0:CAP], T.W[:, 256:384], rhs, True, True)
        st[b]["y"] = sig(mm(Y[:, CAP:2 * CAP], T.W[:, 384:512], rhs, True, True))

    def relu(b):
        X, Y, _ = BK[b]
        o = b * FF * CAP
        need(ve, st[b]["x"])
        st[b]["hv"] = sig(ve.tensor_scalar(T.Hh[:, o:o + 2 * CAP], X[:, 0:2 * CAP], 0.0, None, Op.max))
        need(sc, st[b]["y"])
        st[b]["hs"] = sig(sc.activation(T.Hh[:, o + 2 * CAP:o + 4 * CAP], Y[:, 0:2 * CAP], Fn.Relu))

    def mm2(b):
        Zb = BK[b][2]
        o = b * FF * CAP
        for f in range(FF - 1):
            if f == 0:
                need(pe, st[b]["hv"])
            if f == FF // 2:
                need(pe, st[b]["hs"])
            mm(Zb[:, 0:CAP], T.W[:, 512 + 128 * f:640 + 128 * f], T.Hh[:, o + CAP * f:o + CAP * f + CAP], f == 0, False)
        f = FF - 1
        st[b]["z"] = sig(mm(Zb[:, 0:CAP], T.W[:, 512 + 128 * f:640 + 128 * f], T.Hh[:, o + CAP * f:o + CAP * f + CAP],
                            False, True))

    def out_v(b, dst):
        need(ve, st[b]["z"])
        return sig(ve.tensor_copy(dst, BK[b][2][:, 0:CAP]))

    def out_s(b, dst):
        need(sc, st[b]["z"])
        return sig(sc.activation(dst, BK[b][2][:, 0:CAP], Fn.Copy))

    if rank is None:
        r, a = role[core]
        k0, k1 = pairs[a]
        d0, d1 = helpers[(r + k0) % n][a], helpers[(r + k1) % n][a]
        m0, m1 = _split(topo.mask(core, d0) & topo.mask(core, d1), 2)
        nq = len(_bits(_split(topo.mask(cores[r], core), 4)[a]))
        nb = helpers[r][a + 1 - 2 * (a % 2)]
        lo = 256 * (a % 2)
        g.wait_ge(S.warr, nq)
        nx = send(nb, S.warx, T.W[:, lo:lo + 256], T.W[:, lo:lo + 256], topo.mask(core, nb) & topo.mask(core, d0))
        g.wait_ge(S.farr, nq)
        g.remote_dma_fused([xfer(d0, m0, S.rarr0, T.F[:, 0:CAP], T.R[:, 0:CAP]),
                            xfer(d1, m1, S.rarr1, T.F[:, CAP:2 * CAP], T.R[:, CAP:2 * CAP])], local_sem=S.lsem)
        pe.wait_ge(S.warr, nq)
        pe.wait_ge(S.warx, nx)
        pe.wait_ge(S.rarr0, len(_bits(m0)))
        mm1(0, T.R[:, 0:CAP])
        pe.wait_ge(S.rarr1, len(_bits(m1)))
        mm1(1, T.R[:, CAP:2 * CAP])
        relu(0)
        relu(1)
        pe.wait_ge(S.wars, nq)
        mm2(0)
        mm2(1)
        c0 = out_v(0, T.Yo[:, 0:CAP])
        c1 = out_s(1, T.Yo[:, CAP:2 * CAP])
        need(g, c0)
        send(cores[(r - k0) % n], S.zarr, T.Yo[:, 0:CAP], T.Z[:, CAP * k0:CAP * k0 + CAP])
        need(g, c1)
        send(cores[(r - k1) % n], S.zarr, T.Yo[:, CAP:2 * CAP], T.Z[:, CAP * k1:CAP * k1 + CAP])
        g.wait_ge(S.lsem, cnt["l"])
        return

    r = rank
    H = helpers[r]
    g.sync.dma_start(T.E16[0:16, :], T.ex[:, :]).then_inc(S.exl, 16)
    sc.dma_start(T.W[:, 0:512], T.w1[:, :]).then_inc(S.wl1, 16)
    g.sync.dma_start(T.X[:, :], T.x[:, :]).then_inc(S.xl, 16)
    sc.dma_start(T.W[:, 512:1024], T.w2[:, :]).then_inc(S.wl2, 16)

    i_q = sig(g.iota(T.Qs[:, :], [[-1, 128]], 128, 1))
    i_e = sig(g.iota(T.EI[:, :], [[128, 2], [0, 32]], 0, 1))
    i_d = sig(g.iota(T.Dg[:, :], [[-16, 8], [0, 16]], 0, 1, allow_small_or_imprecise_dtypes=True))
    i_t = sig(g.iota(T.T8[:, :], [[16, 32]], SLOTS, 1, allow_small_or_imprecise_dtypes=True))

    c_dm = sig(ve.memset(T.D[:, 0:SLOTS], 0.0))
    need(ve, i_q)
    c_q = sig(ve.tensor_scalar(T.q15[:, :], T.Qs[:, :], 15, None, Op.bitwise_and))
    c_bn = sig(ve.tensor_scalar(T.Bn[:, :], T.Qs[:, :], 128.0, -1.0, Op.is_ge, Op.mult))
    need(ve, c_q)
    c_sel = sig(ve.tensor_scalar(T.SEL[:, :], T.q15[:, :], 0.0, None, Op.is_equal))
    need(ve, i_e)
    c_et = sig(ve.tensor_scalar(T.EIDT[:, :], T.EI[:, :], 4, None, Op.arith_shift_right))

    ve.wait_ge(S.exl, 16)
    c_e = sig(ve.tensor_copy(T.Ebf[0:16, :], T.E16[0:16, :]))
    need(pe, c_sel, c_e)
    mm(T.B0[:, 0:32], T.SEL[0:16, :], T.Ebf[0:16, :], True, True)
    p0 = sig(mm(T.B0[:, 32:64], T.SEL[0:16, :], T.Ebf[0:16, :], True, True))
    ve.memset(T.MSK[:, 0:32], 1.0).then_inc(S.mk, 1)
    ve.memset(T.MSK[:, 32:33], 0.0).then_inc(S.mk, 1)
    ve.memset(T.MSK[:, 33:64], 1.0).then_inc(S.mk, 1)
    c_ik = sig(ve.tensor_scalar(T.I1k[:, :], T.Qs[:, :], 128.0, 1024.0, Op.is_equal, Op.mult))
    need(ve, i_d)
    c_g16 = sig(ve.tensor_scalar(T.G16[:, :], T.Dg[:, :], 16.0, None, Op.is_ge))
    need(ve, p0, c_et)
    c_o = sig(ve.tensor_tensor(T.O[:, :], T.B0[:, 0:64], T.EIDT[:, :], Op.is_equal))
    c_g0 = sig(ve.tensor_scalar(T.G0[:, :], T.Dg[:, :], 0.0, None, Op.is_ge))
    c_g16n = sig(ve.tensor_scalar(T.G16n[:, :], T.Dg[:, :], 16.0, -1.0, Op.is_ge, Op.mult))
    need(ve, c_o)
    ve.wait_ge(S.mk, 3)
    c_s = sig(ve.tensor_tensor_scan(T.Sc[:, :], T.MSK[:, :], T.O[:, :], 0.0, Op.mult, Op.add))
    c_b1 = sig(ve.tensor_scalar(T.b1[0:16, :], T.E16[0:16, :], float(r), float(SLOTS), Op.is_lt, Op.mult))
    c_b2 = sig(ve.tensor_scalar(T.b2[0:16, :], T.E16[0:16, :], float(CAP), float(-CAP * r), Op.mult, Op.add))
    c_zm = sig(ve.memset(T.Z[:, SLOTS:SLOTS + 8], 0.0))
    need(pe, c_o, c_bn, c_ik, c_g16)
    mm(T.B1[:, 0:64], T.Bn[:, :], T.O[:, :], True, False)
    mm(T.B1[:, 0:64], T.G16[:, :], T.O[:, :], False, False)
    mm(T.B1[:, 0:64], T.I1k[:, :], T.O[:, :], False, False)
    need(pe, c_s, c_g0, c_g16n)
    mm(T.B1[:, 0:64], T.G0[:, :], T.Sc[:, :], False, False)
    p1 = sig(mm(T.B1[:, 0:64], T.G16n[:, :], T.Sc[:, :], False, True))
    need(pe, c_b1, c_b2)
    mm(T.B2[:, 0:32], T.SEL[0:16, :], T.b1[0:16, :], True, False)
    mm(T.B2[:, 0:32], T.SEL[0:16, :], T.b2[0:16, :], False, False)
    need(ve, p1)
    c_1 = sig(ve.tensor_scalar(T.R1[:, :], T.B1[:, 0:64], 1024.0, 0.0, Op.subtract, Op.max))
    c_2 = sig(ve.tensor_scalar(T.R2[:, :], T.B1[:, 0:64], float(1024 + CAP), 4096.0, Op.is_ge, Op.mult))
    need(pe, c_1)
    mm(T.B2[:, 0:32], T.SEL[:, :], T.R1[:, 0:32], False, False)
    mm(T.B2[:, 0:32], T.SEL[:, :], T.R1[:, 32:64], False, False)
    need(pe, c_2)
    mm(T.B2[:, 0:32], T.SEL[:, :], T.R2[:, 0:32], False, False)
    p2 = sig(mm(T.B2[:, 0:32], T.SEL[:, :], T.R2[:, 32:64], False, True))
    need(ve, p2, i_t)
    c_f1 = sig(ve.tensor_tensor(T.off1[:, :], T.B2[:, 0:32], T.T8[:, :], Op.min))
    need(ve, c_f1, c_dm)
    ve.wait_ge(S.xl, 16)
    c_d = sig(ve.tensor_copy(T.D[:, 0:DW].indirect(T.off1[:, 0:32]), T.X[:, :]))
    c_f2 = sig(ve.tensor_scalar(T.off2[:, :], T.off1[:, :], float(SLOTS), None, Op.min))

    twin = cores[(r + kd) % n]
    dm = _split(topo.mask(core, H[0]), 4)
    g.wait_ge(S.wl1, 16)
    g.remote_dma_fused([xfer(H[a], dm[a], S.warr, T.W[:, 256 * (a % 2):256 * (a % 2) + 256],
                             T.W[:, 256 * (a % 2):256 * (a % 2) + 256]) for a in range(4)], local_sem=S.lsem)
    g.wait_ge(S.wl2, 16)
    g.remote_dma_fused([xfer(H[a], dm[a], S.wars, T.W[:, 512:1024], T.W[:, 512:1024]) for a in range(4)],
                       local_sem=S.lsem)
    need(g, c_d)
    g.remote_dma_fused([xfer(H[a], dm[a], S.farr, T.D[:, CAP * pairs[a][0]:CAP * pairs[a][0] + 2 * CAP], T.F[:, :])
                        for a in range(4)], local_sem=S.lsem)
    nt = send(twin, S.rarr1, T.D[:, CAP * kd:CAP * kd + CAP], T.R[:, CAP:2 * CAP])

    pe.wait_ge(S.wl1, 16)
    pe.wait_ge(S.wl2, 16)
    need(pe, c_d)
    mm1(0, T.D[:, 0:CAP])
    relu(0)
    mm2(0)
    c_own = out_v(0, T.Z[:, 0:CAP])
    pe.wait_ge(S.rarr1, nt)
    mm1(1, T.R[:, CAP:2 * CAP])
    relu(1)
    mm2(1)
    c_tw = out_s(1, T.Yo[:, CAP:2 * CAP])
    need(g, c_tw)
    send(cores[(r - kd) % n], S.zarr, T.Yo[:, CAP:2 * CAP], T.Z[:, CAP * kd:CAP * kd + CAP])

    nz = sum(len(_bits(topo.mask(helpers[(r + k) % n][a], core))) for a in range(4) for k in pairs[a])
    nz += len(_bits(topo.mask(twin, core)))
    h = TOK // 2
    need(ve, c_f2, c_own, c_zm)
    ve.wait_ge(S.zarr, nz)
    c_y = sig(ve.tensor_copy(T.Yf[:, 0:h], T.Z[:, 0:SLOTS + 8].indirect(T.off2[:, 0:16])))
    need(sc, c_f2, c_own, c_zm)
    sc.wait_ge(S.zarr, nz)
    s_y = sig(sc.activation(T.Yf[:, h:TOK], T.Z[:, 0:SLOTS + 8].indirect(T.off2[:, 16:32]), Fn.Copy))
    need(g.sync, c_y, s_y)
    g.sync.dma_start(T.y[:, :], T.Yf[:, :]).then_inc(S.st, 16)
    g.wait_ge(S.st, 16)
    g.wait_ge(S.lsem, cnt["l"])
